import numpy as np
import ml_dtypes


def mxq(x, axis, fmt="e4m3"):
    dtype, down = {"e4m3": (ml_dtypes.float8_e4m3fn, 7), "e5m2": (ml_dtypes.float8_e5m2, 14)}[fmt]
    v = np.moveaxis(np.asarray(x, np.float32).astype(ml_dtypes.bfloat16).astype(np.float64), axis, -1)
    blocks = v.reshape(v.shape[:-1] + (-1, 32))
    amax = np.abs(blocks).max(-1, keepdims=True)
    byte = np.maximum(np.where(amax > 0, np.frexp(amax)[1] - 1 + 127, 0) - down, 1)
    scale = np.exp2(byte - 127.0)
    codes = (blocks / scale).astype(np.float32).astype(dtype).astype(np.float64)
    return np.moveaxis((codes * scale).reshape(v.shape), -1, axis)


WIDE = False


def mx_kscale(k):
    if not WIDE:
        return np.ones(k)
    levels = np.array([10, -10, 5, -5, 0])
    if k % 512:
        return np.exp2(np.random.permutation(np.resize(levels, k // 32))).repeat(32)
    a = np.empty((k // 512, 16))
    for p in range(k // 512):
        a[p, :8] = np.random.permutation(np.resize(levels, 8))
        for g in range(8):
            far = levels[np.abs(levels - a[p, g]) >= 10]
            a[p, g + 8] = far[np.random.randint(len(far))]
    return np.exp2(a.ravel()).repeat(32)


def f64(x):
    return np.asarray(x).astype(np.float64)


def striped(idx):
    return np.tile(idx.reshape(-1, 16).T, (8, 1)).astype(np.uint16)


def unstriped(offs):
    return offs[:16].T.reshape(-1).astype(np.int64)


def striped8(idx):
    return np.concatenate([x.reshape(-1, 16).T for x in idx]).astype(np.uint16)


def runs(offs, k):
    lists = np.stack([offs[16 * r : 16 * r + 16].T.reshape(-1) for r in range(8)]).astype(np.int64)
    return lists[np.arange(k) % 512 // 64]


def pack_weight(w):
    k, n = w.shape
    w = f64(np.asarray(w, np.float32).astype(ml_dtypes.bfloat16)).reshape(k // 32, 32, n)
    amax = np.abs(w).max(1)
    byte = np.clip(np.where(amax > 0, np.frexp(amax)[1] - 1 + 127 - 7, 1), 1, 254)
    scaled = (w * np.exp2(127.0 - byte)[:, None, :]).reshape(k, n).astype(np.float32)
    words = np.ascontiguousarray(scaled.reshape(k // 512, 128, 4, n).transpose(0, 1, 3, 2)).astype(ml_dtypes.float8_e4m3fn).view(np.uint8)
    return words, np.ascontiguousarray(byte.astype(np.uint8).reshape(k // 512, 16, n))


def unpack_weight(words, scales):
    g, p, n, _ = words.shape
    vals = np.ascontiguousarray(words).view(ml_dtypes.float8_e4m3fn).astype(np.float64) * np.repeat(np.exp2(scales.astype(np.float64) - 127.0), 8, axis=1)[..., None]
    return vals.transpose(0, 1, 3, 2).reshape(g * 512, n)


E2M1 = np.array([0.0, 0.5, 1.0, 1.5, 2.0, 3.0, 4.0, 6.0, -0.0, -0.5, -1.0, -1.5, -2.0, -3.0, -4.0, -6.0])


def pack_fp4(w):
    k, n = w.shape
    w = f64(np.asarray(w, np.float32).astype(ml_dtypes.bfloat16)).reshape(k // 32, 32, n)
    amax = np.abs(w).max(1)
    mant, ex = np.frexp(amax / 6.0)
    byte = np.clip(np.where(amax > 0, np.where(mant > 0.5, ex, ex - 1) + 127, 1), 1, 254)
    scaled = (w * np.exp2(127.0 - byte)[:, None, :]).reshape(k, n).astype(np.float32)
    c = np.ascontiguousarray(scaled.reshape(k // 512, 128, 4, n).transpose(0, 1, 3, 2)).astype(ml_dtypes.float4_e2m1fn).view(np.uint8) & 0xF
    words = (c[..., 0::2] | (c[..., 1::2] << 4)).reshape(k // 512, 128, 2 * n)
    return np.ascontiguousarray(words), np.ascontiguousarray(byte.astype(np.uint8).reshape(k // 512, 16, n))


def unpack_fp4(words, scales):
    g, _, n = scales.shape
    words = np.ascontiguousarray(words).reshape(g, 128, n, 2)
    nib = np.empty((g, 128, n, 4), np.uint8)
    nib[..., 0::2] = words & 0xF
    nib[..., 1::2] = words >> 4
    vals = E2M1[nib] * np.repeat(np.exp2(scales.astype(np.float64) - 127.0), 8, axis=1)[..., None]
    return vals.transpose(0, 1, 3, 2).reshape(g * 512, n)


def silu(v):
    return v / (1.0 + np.exp(-np.maximum(v, -700.0)))

def planes(y):
    n, m = y.shape
    v = y.astype(np.float32).astype(ml_dtypes.bfloat16).astype(np.float64).reshape(n // 32, 32, m)
    top = np.abs(v).max(1)
    byte = np.clip(np.where(top > 0, np.frexp(top)[1] - 1 + 127 - 7, 1), 1, 254)
    codes = (v * np.exp2(127.0 - byte)[:, None, :]).reshape(n, m).astype(np.float32).astype(ml_dtypes.float8_e4m3fn).view(np.uint8)
    words = codes.reshape(n // 512, 128, 4, m).transpose(0, 1, 3, 2)
    return np.ascontiguousarray(words), np.ascontiguousarray(byte.astype(np.uint8).reshape(n // 512, 16, m))


K, T, S, N, H = 512, 2048, 512, 512, 512


def setup_inputs():
    n = np.random.standard_normal
    s = mx_kscale(K)[:, None]
    u = mx_kscale(H)
    packed_xT = pack_weight(n((K, T)) * s)
    packed_w3 = pack_fp4(n((H, N)) / np.sqrt(H) / u[:, None])
    return {
        "x_words": packed_xT[0],
        "x_scales": packed_xT[1],
        "w1": (n((K, H)) / np.sqrt(K) / s * u).astype(np.float32),
        "w2": (n((H, H)) / np.sqrt(H) / u[:, None] * u).astype(np.float32),
        "res": (2 * n((N, S))).astype(np.float32),
        "w3_words": packed_w3[0],
        "w3_scales": packed_w3[1],
        "offs": striped(np.random.permutation(T)[:S]),
        "s1": striped8(np.stack([np.random.permutation(S) for _ in range(8)])),
        "s2": striped8(np.stack([np.random.permutation(S) for _ in range(8)])),
    }


def reference(x_words, x_scales, w1, w2, res, w3_words, w3_scales, offs, s1, s2):
    xq = unpack_weight(x_words, x_scales)[:, unstriped(offs)]
    y = silu(mxq(f64(w1), 0, "e4m3").T @ xq)
    z = y[np.arange(H)[:, None], runs(s1, H)]
    h = silu(mxq(f64(w2), 0, "e4m3").T @ mxq(z, 0, "e4m3"))
    z2 = h[np.arange(H)[:, None], runs(s2, H)]
    out_0 = f64(res) + (unpack_fp4(w3_words, w3_scales).T @ mxq(z2, 0, "e4m3"))
    return (out_0,) + planes(out_0)

@@ -1,0 +1,212 @@
+from contextlib import ExitStack
+
+import concourse.mybir as mybir
+
+K, T, S, N, H = 512, 2048, 512, 512, 512
+FLOPS = 2 * S * (K * H + H * H + H * N)
+
+F32 = mybir.dt.float32
+BF16 = mybir.dt.bfloat16
+I32 = mybir.dt.int32
+U32 = mybir.dt.uint32
+U16 = mybir.dt.uint16
+U8 = mybir.dt.uint8
+FP8X4 = mybir.dt.float8_e4m3fn_x4
+FP4X4 = mybir.dt.float4_e2m1fn_x4
+SILU = mybir.ActivationFunctionType.Silu
+ADD = mybir.AluOpType.add
+
+P = 128
+PACK = 4
+LANES = 16
+X_CHUNKS = ((0, 256), (256, 256))
+Z_CHUNKS = ((0, 256), (256, 256))
+O_CHUNKS = ((0, 128), (128, 128), (256, 128), (384, 128))
+
+
+def tile_picked_shuf3_silu_po_kernel(
+    tc, x_words, x_scales, w1, w2, res, w3_words, w3_scales, offs, s1, s2, out_0, out_1, out_2
+):
+    nc = tc.nc
+    with ExitStack() as ctx:
+        keep = ctx.enter_context(tc.tile_pool(name="keep", bufs=1))
+        psum = ctx.enter_context(tc.psum_pool(name="psum", bufs=2))
+
+        ring = ctx.enter_context(tc.tile_pool(name="ring", bufs=2))
+
+        def tile(name, shape, dtype, tag=None):
+            return keep.tile(shape, dtype, name=name, tag=tag or name, align_bytes=64)
+
+        def bank(name, t, shape):
+            return psum.tile(shape, F32, name=name, tag="bank%d" % t)
+
+        def load_list(name, src):
+            lst = keep.tile([P, S // LANES], U16, name=name)
+            nc.sync.dma_start(lst[:], src)
+            return lst
+
+        def load_scales(eng, dst, src):
+            for q in range(4):
+                eng.dma_start(dst[32 * q : 32 * q + 4, :].bitcast(I32), src[0, 4 * q : 4 * q + 4, :].bitcast(I32))
+
+        def load_rows(name, src, tag):
+            raw = tile(name, [P, PACK, src.shape[1]], F32, tag)
+            nc.sync.dma_start(raw[:], src.rearrange("(p j) c -> p j c", j=PACK))
+            return raw
+
+        def copy_on(eng, out, in_):
+            if eng == "scalar":
+                nc.scalar.copy(out, in_)
+            else:
+                nc.vector.tensor_copy(out, in_)
+
+        def round_weight(name, raw, pair, eng):
+            dealt = tile(name, [P, 2, P, PACK], BF16)
+            copy_on(
+                eng,
+                dealt[:].rearrange("p t m j -> p m j t"),
+                raw[:].rearrange("p j (m t) -> p m j t", t=PACK)[:, :, :, 2 * pair : 2 * pair + 2],
+            )
+            return dealt
+
+        def quantize(name, values, width):
+            codes = tile(name + "_codes", [P, width], U32)
+            scales = tile(name + "_scales", [P, width], U8)
+            nc.vector.quantize_mx(out=codes[:].bitcast(FP8X4), scales=scales[:], in_=values)
+            return codes, scales
+
+        def interleave(name, planes, width, eng, tag=None):
+            woven = tile(name, [P, width, PACK], BF16, tag)
+            copy_on(
+                eng,
+                woven[:].rearrange("p (c i) t -> p c t i", i=4),
+                planes.rearrange("p t (c i) -> p c t i", i=4),
+            )
+            return woven[:].rearrange("p c t -> p (c t)")
+
+        def shuffle(planes, rows, lst, c0, width):
+            for t in range(PACK):
+                nc.vector.tensor_copy(planes[:, t, :], rows[t][:].indirect(lst[:, c0 // LANES : (c0 + width) // LANES]))
+            return planes
+
+        xs = tile("xs", [P, T], U8, "slot_c")
+        nc.vector.memset(xs[:].bitcast(I32), 0)
+        warm = tile("warm", [P, 16], F32)
+        nc.vector.memset(warm[:], 0.0)
+        warm2 = tile("warm2", [P, 16], F32)
+        offs_t = load_list("offs_t", offs)
+        s1_t = load_list("s1_t", s1)
+        w1_raw = load_rows("w1_raw", w1, "slot_a")
+        load_scales(nc.scalar, xs, x_scales)
+        nc.scalar.activation(warm2[:], warm[:], SILU)
+        xw = tile("xw", [P, T], I32, "slot_b")
+        nc.sync.dma_start(xw[:], x_words[0].rearrange("p c r -> p (c r)").bitcast(I32))
+        w3_raw = tile("w3_raw", [P, 2 * N], U8)
+        nc.sync.dma_start(w3_raw[:].bitcast(I32), w3_words[0].bitcast(I32))
+        s2_t = load_list("s2_t", s2)
+
+        xq_scales = tile("xq_scales", [P, S], U8)
+        nc.vector.tensor_copy(xq_scales[:], xs[:].indirect(offs_t[:]))
+
+        w1_bf = [round_weight("w1_bf0", w1_raw, 0, "vector"), round_weight("w1_bf1", w1_raw, 1, "scalar")]
+        w1_q = [quantize("w1q%d" % u, w1_bf[u][:].rearrange("p t m j -> p (t m j)"), 2 * P) for u in range(2)]
+        w2_raw = load_rows("w2_raw", w2, "slot_a")
+
+        def product(name, wq, codes, scales, width):
+            banks = []
+            for t in range(PACK):
+                acc = bank("%s_%d" % (name, t), t, [P, width])
+                cols = slice((t % 2) * P, (t % 2 + 1) * P)
+                nc.tensor.matmul_mx(
+                    out=acc[:],
+                    lhsT=wq[t // 2][0][:, cols].bitcast(FP8X4),
+                    lhsT_scale=wq[t // 2][1][:, cols],
+                    rhs=codes,
+                    rhs_scale=scales,
+                    start=True,
+                    stop=True,
+                )
+                banks.append(acc)
+            return banks
+
+        y = [tile("y%d" % t, [P, S], F32) for t in range(PACK)]
+        accs = []
+        for c0, width in X_CHUNKS:
+            xq = tile("xq%d" % c0, [P, width], U32, "slot_c" if c0 == 0 else "slot_d")
+            nc.vector.tensor_copy(xq[:], xw[:].bitcast(U32).indirect(offs_t[:, c0 // LANES : (c0 + width) // LANES]))
+            accs.append(product("acc1_%d" % c0, w1_q, xq[:].bitcast(FP8X4), xq_scales[:, c0 : c0 + width], width))
+        for t in range(PACK):
+            for (c0, width), banks in zip(X_CHUNKS, accs):
+                nc.scalar.activation(y[t][:, c0 : c0 + width], banks[t][:], SILU)
+
+        w3_codes = tile("w3_codes", [P, PACK, P, 2], U8)
+        nc.vector.tensor_copy(w3_codes[:].rearrange("p t m b -> p m t b"), w3_raw[:].rearrange("p (m t b) -> p m t b", t=PACK, b=2))
+        w3s_raw = tile("w3s_raw", [P, N], U8, "slot_c")
+        nc.gpsimd.memset(w3s_raw[:].bitcast(I32), 0)
+        load_scales(nc.sync, w3s_raw, w3_scales)
+        res_t = load_rows("res_t", res, "slot_b")
+
+        z_planes = [shuffle(tile("z%d" % c0, [P, PACK, width], BF16), y, s1_t, c0, width) for c0, width in Z_CHUNKS]
+        w2_bf = [round_weight("w2_bf%d" % u, w2_raw, u, "scalar") for u in range(2)]
+        w2_q = [quantize("w2q%d" % u, w2_bf[u][:].rearrange("p t m j -> p (t m j)"), 2 * P) for u in range(2)]
+        h = [tile("h%d" % t, [P, S], F32) for t in range(PACK)]
+        accs = []
+        for n, (c0, width) in enumerate(Z_CHUNKS):
+            woven = interleave("zw%d" % c0, z_planes[n][:], width, "scalar" if n == 0 else "vector", "slot_a" if n == 0 else None)
+            codes, scales = quantize("zq%d" % c0, woven, width)
+            accs.append(product("acc2_%d" % c0, w2_q, codes[:].bitcast(FP8X4), scales[:], width))
+        for t in range(PACK):
+            for (c0, width), banks in zip(Z_CHUNKS, accs):
+                nc.scalar.activation(h[t][:, c0 : c0 + width], banks[t][:], SILU)
+
+        w3_sc = tile("w3_sc", [P, PACK, P], U8, "zw256")
+        nc.vector.tensor_copy(w3_sc[:].rearrange("p t m -> p m t"), w3s_raw[:].rearrange("p (m t) -> p m t", t=PACK))
+
+        o_codes = tile("o_codes", [P, S], U32)
+        o_scales = tile("o_scales", [P, S], U8)
+        out_rows = out_0.rearrange("(p t) c -> p t c", t=PACK)
+        out_words = out_1[0].rearrange("p c r -> p (c r)").bitcast(I32)
+        stage = {}
+
+        def gather3(n):
+            c0, width = O_CHUNKS[n]
+            planes = shuffle(ring.tile([P, PACK, width], BF16, name="z2", align_bytes=64), h, s2_t, c0, width)
+            stage[n] = interleave("z2w%d" % c0, planes[:], width, "scalar")
+
+        def mult3(n):
+            c0, width = O_CHUNKS[n]
+            codes, scales = quantize("z2q%d" % c0, stage[n], width)
+            acc = bank("acc3_%d" % c0, n % PACK, [P, PACK, width])
+            for t in range(PACK):
+                nc.tensor.matmul_mx(
+                    out=acc[:, t, :],
+                    lhsT=w3_codes[:, t, :, :].rearrange("p m b -> p (m b)").bitcast(FP4X4),
+                    lhsT_scale=w3_sc[:, t, :],
+                    rhs=codes[:].bitcast(FP8X4),
+                    rhs_scale=scales[:],
+                    start=True,
+                    stop=True,
+                )
+            stage[n] = acc
+
+        def add3(n):
+            c0, width = O_CHUNKS[n]
+            summed = tile("sum%d" % c0, [P, PACK, width], F32)
+            nc.vector.tensor_tensor(summed[:], stage[n][:], res_t[:, :, c0 : c0 + width], ADD)
+            nc.sync.dma_start(out_rows[:, :, c0 : c0 + width], summed[:])
+            stage[n] = interleave("ow%d" % c0, summed[:], width, "scalar")
+
+        def planes3(n):
+            c0, width = O_CHUNKS[n]
+            cols = slice(c0, c0 + width)
+            nc.vector.quantize_mx(out=o_codes[:, cols].bitcast(FP8X4), scales=o_scales[:, cols], in_=stage[n])
+            nc.sync.dma_start(out_words[:, cols], o_codes[:, cols].bitcast(I32))
+
+        steps = (gather3, mult3, add3, planes3)
+        for tick in range(len(O_CHUNKS) + len(steps) - 1):
+            for depth, step in enumerate(steps):
+                if 0 <= tick - depth < len(O_CHUNKS):
+                    step(tick - depth)
+        for q in range(4):
+            eng = nc.sync if q % 2 == 0 else nc.scalar
+            eng.dma_start(out_2[0, 4 * q : 4 * q + 4, :].bitcast(I32), o_scales[32 * q : 32 * q + 4, :].bitcast(I32))

@@ -19,9 +19,11 @@ ADD = mybir.AluOpType.add
 P = 128
 PACK = 4
 LANES = 16
-X_CHUNKS = ((0, 256), (256, 256))
+BANK = 512
+W1_CHUNKS = ((0, 256), (256, 128), (384, 128))
+W2_CHUNKS = ((0, 256), (256, 256))
 Z_CHUNKS = ((0, 256), (256, 256))
-O_CHUNKS = ((0, 128), (128, 128), (256, 128), (384, 128))
+O_CHUNKS = ((0, 256), (256, 128), (384, 128))
 
 
 def tile_picked_shuf3_silu_po_kernel(
@@ -31,8 +33,6 @@ def tile_picked_shuf3_silu_po_kernel(
     with ExitStack() as ctx:
         keep = ctx.enter_context(tc.tile_pool(name="keep", bufs=1))
         psum = ctx.enter_context(tc.psum_pool(name="psum", bufs=2))
-
-        ring = ctx.enter_context(tc.tile_pool(name="ring", bufs=2))
 
         def tile(name, shape, dtype, tag=None):
             return keep.tile(shape, dtype, name=name, tag=tag or name, align_bytes=64)
@@ -49,68 +49,47 @@ def tile_picked_shuf3_silu_po_kernel(
             for q in range(4):
                 eng.dma_start(dst[32 * q : 32 * q + 4, :].bitcast(I32), src[0, 4 * q : 4 * q + 4, :].bitcast(I32))
 
-        def load_rows(name, src, tag):
-            raw = tile(name, [P, PACK, src.shape[1]], F32, tag)
-            nc.sync.dma_start(raw[:], src.rearrange("(p j) c -> p j c", j=PACK))
+        def load_rows(name, src, c0, width, tag):
+            raw = tile(name, [P, PACK, width], F32, tag)
+            nc.sync.dma_start(raw[:], src.rearrange("(p j) c -> p j c", j=PACK)[:, :, c0 : c0 + width])
             return raw
 
-        def copy_on(eng, out, in_):
-            if eng == "scalar":
-                nc.scalar.copy(out, in_)
-            else:
-                nc.vector.tensor_copy(out, in_)
-
-        def round_weight(name, raw, pair, eng):
-            dealt = tile(name, [P, 2, P, PACK], BF16)
-            copy_on(
-                eng,
-                dealt[:].rearrange("p t m j -> p m j t"),
-                raw[:].rearrange("p j (m t) -> p m j t", t=PACK)[:, :, :, 2 * pair : 2 * pair + 2],
+        def round_weight(copy, dealt, raw, c0, width, t0, t1):
+            copy(
+                dealt[:].rearrange("p t m j -> p m j t")[:, c0 // PACK : (c0 + width) // PACK, :, :],
+                raw[:].rearrange("p j (m t) -> p m j t", t=PACK)[:, :, :, t0:t1],
             )
-            return dealt
 
-        def quantize(name, values, width):
-            codes = tile(name + "_codes", [P, width], U32)
+        def quantize(name, values, width, tag=None):
+            codes = tile(name + "_codes", [P, width], U32, tag)
             scales = tile(name + "_scales", [P, width], U8)
             nc.vector.quantize_mx(out=codes[:].bitcast(FP8X4), scales=scales[:], in_=values)
             return codes, scales
 
-        def interleave(name, planes, width, eng, tag=None):
+        def quantize_weight(name, dealt):
+            return [
+                quantize("%s%d" % (name, u), dealt[:, 2 * u : 2 * u + 2, :, :].rearrange("p t m j -> p (t m j)"), 2 * P)
+                for u in range(2)
+            ]
+
+        def interleave(copies, name, planes, width, tag=None):
             woven = tile(name, [P, width, PACK], BF16, tag)
-            copy_on(
-                eng,
-                woven[:].rearrange("p (c i) t -> p c t i", i=4),
-                planes.rearrange("p t (c i) -> p c t i", i=4),
-            )
+            share = width // len(copies)
+            for n, copy in enumerate(copies):
+                cols = slice(n * share, (n + 1) * share)
+                copy(
+                    woven[:, cols, :].rearrange("p (c i) t -> p c t i", i=4),
+                    planes[:, :, cols].rearrange("p t (c i) -> p c t i", i=4),
+                )
             return woven[:].rearrange("p c t -> p (c t)")
 
-        def shuffle(planes, rows, lst, c0, width):
+        def shuffle(name, rows, lst, chunks, tag=None):
+            planes = [tile("%s%d" % (name, c0), [P, PACK, width], BF16, tag) for c0, width in chunks]
             for t in range(PACK):
-                nc.vector.tensor_copy(planes[:, t, :], rows[t][:].indirect(lst[:, c0 // LANES : (c0 + width) // LANES]))
+                for n, (c0, width) in enumerate(chunks):
+                    window = rows[t][:].indirect(lst[:, c0 // LANES : (c0 + width) // LANES])
+                    nc.vector.tensor_copy(planes[n][:, t, :], window)
             return planes
-
-        xs = tile("xs", [P, T], U8, "slot_c")
-        nc.vector.memset(xs[:].bitcast(I32), 0)
-        warm = tile("warm", [P, 16], F32)
-        nc.vector.memset(warm[:], 0.0)
-        warm2 = tile("warm2", [P, 16], F32)
-        offs_t = load_list("offs_t", offs)
-        s1_t = load_list("s1_t", s1)
-        w1_raw = load_rows("w1_raw", w1, "slot_a")
-        load_scales(nc.scalar, xs, x_scales)
-        nc.scalar.activation(warm2[:], warm[:], SILU)
-        xw = tile("xw", [P, T], I32, "slot_b")
-        nc.sync.dma_start(xw[:], x_words[0].rearrange("p c r -> p (c r)").bitcast(I32))
-        w3_raw = tile("w3_raw", [P, 2 * N], U8)
-        nc.sync.dma_start(w3_raw[:].bitcast(I32), w3_words[0].bitcast(I32))
-        s2_t = load_list("s2_t", s2)
-
-        xq_scales = tile("xq_scales", [P, S], U8)
-        nc.vector.tensor_copy(xq_scales[:], xs[:].indirect(offs_t[:]))
-
-        w1_bf = [round_weight("w1_bf0", w1_raw, 0, "vector"), round_weight("w1_bf1", w1_raw, 1, "scalar")]
-        w1_q = [quantize("w1q%d" % u, w1_bf[u][:].rearrange("p t m j -> p (t m j)"), 2 * P) for u in range(2)]
-        w2_raw = load_rows("w2_raw", w2, "slot_a")
 
         def product(name, wq, codes, scales, width):
             banks = []
@@ -129,57 +108,94 @@ def tile_picked_shuf3_silu_po_kernel(
                 banks.append(acc)
             return banks
 
-        y = [tile("y%d" % t, [P, S], F32) for t in range(PACK)]
-        accs = []
-        for c0, width in X_CHUNKS:
-            xq = tile("xq%d" % c0, [P, width], U32, "slot_c" if c0 == 0 else "slot_d")
-            nc.vector.tensor_copy(xq[:], xw[:].bitcast(U32).indirect(offs_t[:, c0 // LANES : (c0 + width) // LANES]))
-            accs.append(product("acc1_%d" % c0, w1_q, xq[:].bitcast(FP8X4), xq_scales[:, c0 : c0 + width], width))
-        for t in range(PACK):
-            for (c0, width), banks in zip(X_CHUNKS, accs):
-                nc.scalar.activation(y[t][:, c0 : c0 + width], banks[t][:], SILU)
+        on_scalar, on_vector = nc.scalar.copy, nc.vector.tensor_copy
 
-        w3_codes = tile("w3_codes", [P, PACK, P, 2], U8)
-        nc.vector.tensor_copy(w3_codes[:].rearrange("p t m b -> p m t b"), w3_raw[:].rearrange("p (m t b) -> p m t b", t=PACK, b=2))
-        w3s_raw = tile("w3s_raw", [P, N], U8, "slot_c")
-        nc.gpsimd.memset(w3s_raw[:].bitcast(I32), 0)
+        xs = tile("xs", [P, T], U8, "xs")
+        nc.vector.memset(xs[:].bitcast(I32), 0)
+        warm_in = [tile("warm_in%d" % n, [P, 16], F32, "w1_raw%d" % n) for n in range(2)]
+        for n in range(2):
+            nc.vector.memset(warm_in[n][:], 0.0)
+        warm_out = tile("warm_out", [P, 16], F32, "w1_raw2")
+        zero = tile("zero", [P, 16], F32, "late")
+        nc.vector.memset(zero[:], 0.0)
+        offs_t = load_list("offs_t", offs)
+        xw = tile("xw", [P, T], I32, "xw")
+        nc.sync.dma_start(xw[:], x_words[0].rearrange("p c r -> p (c r)").bitcast(I32))
+        load_scales(nc.sync, xs, x_scales)
+        nc.scalar.activation(warm_out[:], warm_in[0][:], SILU, bias=warm_in[1][:, 0:1])
+        w1_raw = [load_rows("w1_raw%d" % n, w1, c0, width, None) for n, (c0, width) in enumerate(W1_CHUNKS)]
+        s1_t = load_list("s1_t", s1)
+        s2_t = load_list("s2_t", s2)
+
+        xq_scales = tile("xq_scales", [P, S], U8)
+        nc.vector.tensor_copy(xq_scales[:], xs[:].indirect(offs_t[:]))
+        xq = tile("xq", [P, S], U32)
+        nc.vector.tensor_copy(xq[:], xw[:].bitcast(U32).indirect(offs_t[:]))
+
+        w3s_raw = tile("w3s_raw", [P, N], U8, "xs")
+        nc.vector.memset(w3s_raw[:].bitcast(I32), 0)
         load_scales(nc.sync, w3s_raw, w3_scales)
-        res_t = load_rows("res_t", res, "slot_b")
+        w2_raw = [load_rows("w2_raw0", w2, 0, 256, "xw")]
 
-        z_planes = [shuffle(tile("z%d" % c0, [P, PACK, width], BF16), y, s1_t, c0, width) for c0, width in Z_CHUNKS]
-        w2_bf = [round_weight("w2_bf%d" % u, w2_raw, u, "scalar") for u in range(2)]
-        w2_q = [quantize("w2q%d" % u, w2_bf[u][:].rearrange("p t m j -> p (t m j)"), 2 * P) for u in range(2)]
-        h = [tile("h%d" % t, [P, S], F32) for t in range(PACK)]
-        accs = []
-        for n, (c0, width) in enumerate(Z_CHUNKS):
-            woven = interleave("zw%d" % c0, z_planes[n][:], width, "scalar" if n == 0 else "vector", "slot_a" if n == 0 else None)
-            codes, scales = quantize("zq%d" % c0, woven, width)
-            accs.append(product("acc2_%d" % c0, w2_q, codes[:].bitcast(FP8X4), scales[:], width))
-        for t in range(PACK):
-            for (c0, width), banks in zip(Z_CHUNKS, accs):
-                nc.scalar.activation(h[t][:, c0 : c0 + width], banks[t][:], SILU)
+        w1_bf = [tile("w1_bf%d" % u, [P, 2, P, PACK], BF16) for u in range(2)]
+        for raw, (c0, width) in zip(w1_raw, W1_CHUNKS):
+            round_weight(on_scalar, w1_bf[0], raw, c0, width, 0, 2)
+            round_weight(on_vector, w1_bf[1], raw, c0, width, 2, 4)
+        w1_q = [quantize("w1q%d" % u, w1_bf[u][:].rearrange("p t m j -> p (t m j)"), 2 * P, (None, "w1_bf0")[u]) for u in range(2)]
 
-        w3_sc = tile("w3_sc", [P, PACK, P], U8, "zw256")
+        w3_raw = tile("w3_raw", [P, 2 * N], U8, "w1_raw0")
+        nc.sync.dma_start(w3_raw[:].bitcast(I32), w3_words[0].bitcast(I32))
+        w2_raw.append(load_rows("w2_raw1", w2, 256, 256, "w1_raw1"))
+        res_t = load_rows("res_t", res, 0, S, "w1_raw2")
+
+        y = [tile("y%d" % t, [P, S], F32) for t in range(PACK)]
+        for t, acc in enumerate(product("acc1", w1_q, xq[:].bitcast(FP8X4), xq_scales[:], S)):
+            nc.scalar.activation(y[t][:], acc[:], SILU)
+
+        w3_sc = tile("w3_sc", [P, PACK, P], U8, "w1_bf1")
         nc.vector.tensor_copy(w3_sc[:].rearrange("p t m -> p m t"), w3s_raw[:].rearrange("p (m t) -> p m t", t=PACK))
+
+        z_planes = shuffle("z", y, s1_t, Z_CHUNKS)
+        w2_bf = tile("w2_bf", [P, PACK, P, PACK], BF16)
+        for raw, (c0, width) in zip(w2_raw, W2_CHUNKS):
+            round_weight(on_scalar, w2_bf, raw, c0, width, 0, 4)
+        w2_q = quantize_weight("w2q", w2_bf)
+        h = [tile("h%d" % t, [P, S], F32) for t in range(PACK)]
+        accs = {}
+        for n in (0, 1):
+            woven = interleave(([on_scalar], [on_vector, on_scalar])[n], "zw%d" % n, z_planes[n], 256, ("xw", "w1_raw1")[n])
+            codes, scales = quantize("zq%d" % n, woven, 256)
+            accs[n] = product("acc2_%d" % n, w2_q, codes[:].bitcast(FP8X4), scales[:], 256)
+        for t in range(PACK):
+            for n in (0, 1):
+                last = t == PACK - 1 and n == 1
+                nc.scalar.activation(h[t][:, 256 * n : 256 * n + 256], accs[n][t][:], SILU, bias=zero[:, 0:1] if last else 0.0)
+
+        w3_codes = tile("w3_codes", [P, PACK, P, 2], U8, "w1_raw1")
+        nc.vector.tensor_copy(w3_codes[:].rearrange("p t m b -> p m t b"), w3_raw[:].rearrange("p (m t b) -> p m t b", t=PACK, b=2))
 
         o_codes = tile("o_codes", [P, S], U32)
         o_scales = tile("o_scales", [P, S], U8)
         out_rows = out_0.rearrange("(p t) c -> p t c", t=PACK)
         out_words = out_1[0].rearrange("p c r -> p (c r)").bitcast(I32)
         stage = {}
+        used = [0]
 
         def gather3(n):
-            c0, width = O_CHUNKS[n]
-            planes = shuffle(ring.tile([P, PACK, width], BF16, name="z2", align_bytes=64), h, s2_t, c0, width)
-            stage[n] = interleave("z2w%d" % c0, planes[:], width, "scalar")
+            planes = shuffle("z2_", h, s2_t, O_CHUNKS[n : n + 1], (None, "late", "z2w0")[n])
+            stage[n] = interleave([on_scalar], "z2w%d" % n, planes[0], O_CHUNKS[n][1])
 
         def mult3(n):
             c0, width = O_CHUNKS[n]
             codes, scales = quantize("z2q%d" % c0, stage[n], width)
-            acc = bank("acc3_%d" % c0, n % PACK, [P, PACK, width])
+            per_bank = BANK // width
+            banks = []
             for t in range(PACK):
+                if t % per_bank == 0:
+                    banks.append(bank("acc3_%d_%d" % (n, t), len(used) - 1, [P, per_bank, width]))
+                    used.append(0)
                 nc.tensor.matmul_mx(
-                    out=acc[:, t, :],
+                    out=banks[-1][:, t % per_bank, :],
                     lhsT=w3_codes[:, t, :, :].rearrange("p m b -> p (m b)").bitcast(FP4X4),
                     lhsT_scale=w3_sc[:, t, :],
                     rhs=codes[:].bitcast(FP8X4),
@@ -187,14 +203,17 @@ def tile_picked_shuf3_silu_po_kernel(
                     start=True,
                     stop=True,
                 )
-            stage[n] = acc
+            stage[n] = banks
 
         def add3(n):
             c0, width = O_CHUNKS[n]
+            per_bank = BANK // width
             summed = tile("sum%d" % c0, [P, PACK, width], F32)
-            nc.vector.tensor_tensor(summed[:], stage[n][:], res_t[:, :, c0 : c0 + width], ADD)
+            for b, acc in enumerate(stage[n]):
+                rows = slice(b * per_bank, (b + 1) * per_bank)
+                nc.vector.tensor_tensor(summed[:, rows, :], acc[:], res_t[:, rows, c0 : c0 + width], ADD)
             nc.sync.dma_start(out_rows[:, :, c0 : c0 + width], summed[:])
-            stage[n] = interleave("ow%d" % c0, summed[:], width, "scalar")
+            stage[n] = interleave([on_scalar], "ow%d" % c0, summed, width)
 
         def planes3(n):
             c0, width = O_CHUNKS[n]
@@ -202,11 +221,17 @@ def tile_picked_shuf3_silu_po_kernel(
             nc.vector.quantize_mx(out=o_codes[:, cols].bitcast(FP8X4), scales=o_scales[:, cols], in_=stage[n])
             nc.sync.dma_start(out_words[:, cols], o_codes[:, cols].bitcast(I32))
 
-        steps = (gather3, mult3, add3, planes3)
-        for tick in range(len(O_CHUNKS) + len(steps) - 1):
-            for depth, step in enumerate(steps):
-                if 0 <= tick - depth < len(O_CHUNKS):
-                    step(tick - depth)
+        gather3(0)
+        gather3(1)
+        mult3(0)
+        gather3(2)
+        mult3(1)
+        add3(0)
+        mult3(2)
+        add3(1)
+        add3(2)
+        for n in range(3):
+            planes3(n)
         for q in range(4):
             eng = nc.sync if q % 2 == 0 else nc.scalar
             eng.dma_start(out_2[0, 4 * q : 4 * q + 4, :].bitcast(I32), o_scales[32 * q : 32 * q + 4, :].bitcast(I32))

@@ -72,15 +72,12 @@ def tile_picked_shuf3_silu_po_kernel(
                 for u in range(2)
             ]
 
-        def interleave(copies, name, planes, width, tag=None):
-            woven = tile(name, [P, width, PACK], BF16, tag)
-            share = width // len(copies)
-            for n, copy in enumerate(copies):
-                cols = slice(n * share, (n + 1) * share)
-                copy(
-                    woven[:, cols, :].rearrange("p (c i) t -> p c t i", i=4),
-                    planes[:, :, cols].rearrange("p t (c i) -> p c t i", i=4),
-                )
+        def weave(copy, woven, planes):
+            copy(woven.rearrange("p (c i) t -> p c t i", i=4), planes.rearrange("p t (c i) -> p c t i", i=4))
+
+        def interleave(name, planes, width):
+            woven = tile(name, [P, width, PACK], BF16)
+            weave(on_scalar, woven[:], planes[:])
             return woven[:].rearrange("p c t -> p (c t)")
 
         def shuffle(name, rows, lst, chunks, tag=None):
@@ -91,50 +88,47 @@ def tile_picked_shuf3_silu_po_kernel(
                     nc.vector.tensor_copy(planes[n][:, t, :], window)
             return planes
 
-        def product(name, wq, codes, scales, width):
-            banks = []
-            for t in range(PACK):
-                acc = bank("%s_%d" % (name, t), t, [P, width])
-                cols = slice((t % 2) * P, (t % 2 + 1) * P)
-                nc.tensor.matmul_mx(
-                    out=acc[:],
-                    lhsT=wq[t // 2][0][:, cols].bitcast(FP8X4),
-                    lhsT_scale=wq[t // 2][1][:, cols],
-                    rhs=codes,
-                    rhs_scale=scales,
-                    start=True,
-                    stop=True,
-                )
-                banks.append(acc)
-            return banks
+        def product(acc, wq, t, codes, scales):
+            cols = slice((t % 2) * P, (t % 2 + 1) * P)
+            nc.tensor.matmul_mx(
+                out=acc,
+                lhsT=wq[t // 2][0][:, cols].bitcast(FP8X4),
+                lhsT_scale=wq[t // 2][1][:, cols],
+                rhs=codes[:].bitcast(FP8X4),
+                rhs_scale=scales[:],
+                start=True,
+                stop=True,
+            )
 
         on_scalar, on_vector = nc.scalar.copy, nc.vector.tensor_copy
 
         xs = tile("xs", [P, T], U8, "xs")
         nc.vector.memset(xs[:].bitcast(I32), 0)
-        warm_in = [tile("warm_in%d" % n, [P, 16], F32, "w1_raw%d" % n) for n in range(2)]
-        for n in range(2):
+        warm_in = [tile("warm_in%d" % n, [P, 16], F32, ("w1_raw0", "w1_raw1", "w3s_raw")[n]) for n in range(3)]
+        for n in range(3):
             nc.vector.memset(warm_in[n][:], 0.0)
         warm_out = tile("warm_out", [P, 16], F32, "w1_raw2")
-        zero = tile("zero", [P, 16], F32, "late")
-        nc.vector.memset(zero[:], 0.0)
+        zero = [tile("zero%d" % n, [P, 16], F32, "late%d" % n) for n in range(2)]
+        for n in range(2):
+            nc.vector.memset(zero[n][:], 0.0)
         offs_t = load_list("offs_t", offs)
+        s1_t = load_list("s1_t", s1)
         xw = tile("xw", [P, T], I32, "xw")
         nc.sync.dma_start(xw[:], x_words[0].rearrange("p c r -> p (c r)").bitcast(I32))
         load_scales(nc.sync, xs, x_scales)
-        nc.scalar.activation(warm_out[:], warm_in[0][:], SILU, bias=warm_in[1][:, 0:1])
+        nc.scalar.activation(warm_out[:], warm_in[0][:], SILU, bias=warm_in[1][:, 0:1], scale=warm_in[2][:, 0:1])
         w1_raw = [load_rows("w1_raw%d" % n, w1, c0, width, None) for n, (c0, width) in enumerate(W1_CHUNKS)]
-        s1_t = load_list("s1_t", s1)
         s2_t = load_list("s2_t", s2)
+
+        w3s_raw = tile("w3s_raw", [P, N], U8)
+        nc.vector.memset(w3s_raw[:].bitcast(I32), 0)
+        load_scales(nc.sync, w3s_raw, w3_scales)
 
         xq_scales = tile("xq_scales", [P, S], U8)
         nc.vector.tensor_copy(xq_scales[:], xs[:].indirect(offs_t[:]))
         xq = tile("xq", [P, S], U32)
         nc.vector.tensor_copy(xq[:], xw[:].bitcast(U32).indirect(offs_t[:]))
 
-        w3s_raw = tile("w3s_raw", [P, N], U8, "xs")
-        nc.vector.memset(w3s_raw[:].bitcast(I32), 0)
-        load_scales(nc.sync, w3s_raw, w3_scales)
         w2_raw = [load_rows("w2_raw0", w2, 0, 256, "xw")]
 
         w1_bf = [tile("w1_bf%d" % u, [P, 2, P, PACK], BF16) for u in range(2)]
@@ -143,35 +137,37 @@ def tile_picked_shuf3_silu_po_kernel(
             round_weight(on_vector, w1_bf[1], raw, c0, width, 2, 4)
         w1_q = [quantize("w1q%d" % u, w1_bf[u][:].rearrange("p t m j -> p (t m j)"), 2 * P, (None, "w1_bf0")[u]) for u in range(2)]
 
-        w3_raw = tile("w3_raw", [P, 2 * N], U8, "w1_raw0")
-        nc.sync.dma_start(w3_raw[:].bitcast(I32), w3_words[0].bitcast(I32))
-        w2_raw.append(load_rows("w2_raw1", w2, 256, 256, "w1_raw1"))
-        res_t = load_rows("res_t", res, 0, S, "w1_raw2")
+        w2_raw.append(load_rows("w2_raw1", w2, 256, 256, "w1_raw0"))
 
         y = [tile("y%d" % t, [P, S], F32) for t in range(PACK)]
-        for t, acc in enumerate(product("acc1", w1_q, xq[:].bitcast(FP8X4), xq_scales[:], S)):
-            nc.scalar.activation(y[t][:], acc[:], SILU)
+        for t in range(PACK):
+            acc = bank("acc1_%d" % t, t, [P, S])
+            product(acc[:], w1_q, t, xq, xq_scales)
+            nc.scalar.activation(y[t][:], acc[:], SILU, bias=zero[0][:, 0:1] if t == PACK - 1 else 0.0)
 
+        w3_raw = tile("w3_raw", [P, 2 * N], U8, "w1q0_codes")
+        nc.sync.dma_start(w3_raw[:].bitcast(I32), w3_words[0].bitcast(I32))
+        res_t = load_rows("res_t", res, 0, S, "xq")
         w3_sc = tile("w3_sc", [P, PACK, P], U8, "w1_bf1")
         nc.vector.tensor_copy(w3_sc[:].rearrange("p t m -> p m t"), w3s_raw[:].rearrange("p (m t) -> p m t", t=PACK))
 
-        z_planes = shuffle("z", y, s1_t, Z_CHUNKS)
+        z_planes = shuffle("z", y, s1_t, Z_CHUNKS[0:1]) + shuffle("z", y, s1_t, Z_CHUNKS[1:2], "late0")
         w2_bf = tile("w2_bf", [P, PACK, P, PACK], BF16)
         for raw, (c0, width) in zip(w2_raw, W2_CHUNKS):
             round_weight(on_scalar, w2_bf, raw, c0, width, 0, 4)
         w2_q = quantize_weight("w2q", w2_bf)
         h = [tile("h%d" % t, [P, S], F32) for t in range(PACK)]
-        accs = {}
-        for n in (0, 1):
-            woven = interleave(([on_scalar], [on_vector, on_scalar])[n], "zw%d" % n, z_planes[n], 256, ("xw", "w1_raw1")[n])
-            codes, scales = quantize("zq%d" % n, woven, 256)
-            accs[n] = product("acc2_%d" % n, w2_q, codes[:].bitcast(FP8X4), scales[:], 256)
+        woven = tile("zw", [P, S, PACK], BF16, "w1_raw0")
+        weave(on_scalar, woven[:, 0:256, :], z_planes[0][:])
+        weave(on_vector, woven[:, 256:384, :], z_planes[1][:, :, 0:128])
+        weave(on_scalar, woven[:, 384:512, :], z_planes[1][:, :, 128:256])
+        zq, zq_scales = quantize("zq", woven[:].rearrange("p c t -> p (c t)"), S)
         for t in range(PACK):
-            for n in (0, 1):
-                last = t == PACK - 1 and n == 1
-                nc.scalar.activation(h[t][:, 256 * n : 256 * n + 256], accs[n][t][:], SILU, bias=zero[:, 0:1] if last else 0.0)
+            acc = bank("acc2_%d" % t, t, [P, S])
+            product(acc[:], w2_q, t, zq, zq_scales)
+            nc.scalar.activation(h[t][:], acc[:], SILU, bias=zero[1][:, 0:1] if t == PACK - 1 else 0.0)
 
-        w3_codes = tile("w3_codes", [P, PACK, P, 2], U8, "w1_raw1")
+        w3_codes = tile("w3_codes", [P, PACK, P, 2], U8, "w1_raw0")
         nc.vector.tensor_copy(w3_codes[:].rearrange("p t m b -> p m t b"), w3_raw[:].rearrange("p (m t b) -> p m t b", t=PACK, b=2))
 
         o_codes = tile("o_codes", [P, S], U32)
@@ -182,8 +178,8 @@ def tile_picked_shuf3_silu_po_kernel(
         used = [0]
 
         def gather3(n):
-            planes = shuffle("z2_", h, s2_t, O_CHUNKS[n : n + 1], (None, "late", "z2w0")[n])
-            stage[n] = interleave([on_scalar], "z2w%d" % n, planes[0], O_CHUNKS[n][1])
+            planes = shuffle("z2_", h, s2_t, O_CHUNKS[n : n + 1], (None, "late1", "z2w0")[n])
+            stage[n] = interleave("z2w%d" % n, planes[0], O_CHUNKS[n][1])
 
         def mult3(n):
             c0, width = O_CHUNKS[n]
@@ -213,7 +209,7 @@ def tile_picked_shuf3_silu_po_kernel(
                 rows = slice(b * per_bank, (b + 1) * per_bank)
                 nc.vector.tensor_tensor(summed[:, rows, :], acc[:], res_t[:, rows, c0 : c0 + width], ADD)
             nc.sync.dma_start(out_rows[:, :, c0 : c0 + width], summed[:])
-            stage[n] = interleave([on_scalar], "ow%d" % c0, summed, width)
+            stage[n] = interleave("ow%d" % c0, summed, width)
 
         def planes3(n):
             c0, width = O_CHUNKS[n]

@@ -18,216 +18,207 @@ ADD = mybir.AluOpType.add
 
 P = 128
 PACK = 4
-LANES = 16
+GROUP = 16
+QUADRANT = 32
 BANK = 512
-W1_CHUNKS = ((0, 256), (256, 128), (384, 128))
-W2_CHUNKS = ((0, 256), (256, 256))
-Z_CHUNKS = ((0, 256), (256, 256))
-O_CHUNKS = ((0, 256), (256, 128), (384, 128))
+HALVES = (slice(0, S // 2), slice(S // 2, S))
+CHUNKS = (slice(0, 256), slice(256, 384), slice(384, 512))
 
 
 def tile_picked_shuf3_silu_po_kernel(
     tc, x_words, x_scales, w1, w2, res, w3_words, w3_scales, offs, s1, s2, out_0, out_1, out_2
 ):
     nc = tc.nc
+    on_scalar, on_vector = nc.scalar.copy, nc.vector.tensor_copy
     with ExitStack() as ctx:
         keep = ctx.enter_context(tc.tile_pool(name="keep", bufs=1))
         psum = ctx.enter_context(tc.psum_pool(name="psum", bufs=2))
 
-        def tile(name, shape, dtype, tag=None):
-            return keep.tile(shape, dtype, name=name, tag=tag or name, align_bytes=64)
+        def tile(name, shape, dtype, after=None):
+            return keep.tile(shape, dtype, name=name, tag=after or name, align_bytes=64)
 
-        def bank(name, t, shape):
-            return psum.tile(shape, F32, name=name, tag="bank%d" % t)
+        def bank(name, tag, shape):
+            return psum.tile(shape, F32, name=name, tag="bank%d" % tag)
+
+        def entries(lst, cols):
+            return lst[:, cols.start // GROUP : cols.stop // GROUP]
 
         def load_list(name, src):
-            lst = keep.tile([P, S // LANES], U16, name=name)
+            lst = keep.tile([P, S // GROUP], U16, name=name)
             nc.sync.dma_start(lst[:], src)
             return lst
 
-        def load_scales(eng, dst, src):
-            for q in range(4):
-                eng.dma_start(dst[32 * q : 32 * q + 4, :].bitcast(I32), src[0, 4 * q : 4 * q + 4, :].bitcast(I32))
+        def load_rows(name, src, after):
+            rows = tile(name, [P, PACK, src.shape[1]], F32, after)
+            nc.sync.dma_start(rows[:], src.rearrange("(p j) c -> p j c", j=PACK))
+            return rows
 
-        def load_rows(name, src, c0, width, tag):
-            raw = tile(name, [P, PACK, width], F32, tag)
-            nc.sync.dma_start(raw[:], src.rearrange("(p j) c -> p j c", j=PACK)[:, :, c0 : c0 + width])
-            return raw
+        def load_scales(name, src):
+            planes = tile(name, [P, src.shape[2]], U8)
+            nc.vector.memset(planes[:].bitcast(I32), 0)
+            for q in range(P // QUADRANT):
+                live = planes[QUADRANT * q : QUADRANT * q + PACK, :]
+                nc.sync.dma_start(live.bitcast(I32), src[0, PACK * q : PACK * q + PACK, :].bitcast(I32))
+            return planes
 
-        def round_weight(copy, dealt, raw, c0, width, t0, t1):
-            copy(
-                dealt[:].rearrange("p t m j -> p m j t")[:, c0 // PACK : (c0 + width) // PACK, :, :],
-                raw[:].rearrange("p j (m t) -> p m j t", t=PACK)[:, :, :, t0:t1],
-            )
+        def deal_weight(copy, dealt, rows, tiles):
+            copy(dealt.rearrange("p t m j -> p m j t"), rows.rearrange("p j (m t) -> p m j t", t=PACK)[:, :, :, tiles])
 
-        def quantize(name, values, width, tag=None):
-            codes = tile(name + "_codes", [P, width], U32, tag)
-            scales = tile(name + "_scales", [P, width], U8)
-            nc.vector.quantize_mx(out=codes[:].bitcast(FP8X4), scales=scales[:], in_=values)
-            return codes, scales
+        def packed(name, width, after=None):
+            return tile(name + "_codes", [P, width], U32, after), tile(name + "_scales", [P, width], U8)
 
-        def quantize_weight(name, dealt):
-            return [
-                quantize("%s%d" % (name, u), dealt[:, 2 * u : 2 * u + 2, :, :].rearrange("p t m j -> p (t m j)"), 2 * P)
-                for u in range(2)
-            ]
+        def quantize(operand, cols, values):
+            nc.vector.quantize_mx(out=operand[0][:, cols].bitcast(FP8X4), scales=operand[1][:, cols], in_=values)
+
+        def shuffle(name, rows, lst, cols, after=None):
+            planes = tile(name, [P, PACK, cols.stop - cols.start], BF16, after)
+            for t in range(PACK):
+                nc.vector.tensor_copy(planes[:, t, :], rows[t][:].indirect(entries(lst, cols)))
+            return planes
 
         def weave(copy, woven, planes):
             copy(woven.rearrange("p (c i) t -> p c t i", i=4), planes.rearrange("p t (c i) -> p c t i", i=4))
 
-        def interleave(name, planes, width):
-            woven = tile(name, [P, width, PACK], BF16)
-            weave(on_scalar, woven[:], planes[:])
-            return woven[:].rearrange("p c t -> p (c t)")
+        def flat(woven):
+            return woven.rearrange("p c t -> p (c t)")
 
-        def shuffle(name, rows, lst, chunks, tag=None):
-            planes = [tile("%s%d" % (name, c0), [P, PACK, width], BF16, tag) for c0, width in chunks]
+        def hidden_layer(name, weights, moving, last_bias):
+            rows = [tile("%s%d" % (name, t), [P, S], F32) for t in range(PACK)]
             for t in range(PACK):
-                for n, (c0, width) in enumerate(chunks):
-                    window = rows[t][:].indirect(lst[:, c0 // LANES : (c0 + width) // LANES])
-                    nc.vector.tensor_copy(planes[n][:, t, :], window)
-            return planes
+                pair, ms = weights[t // 2], slice((t % 2) * P, (t % 2 + 1) * P)
+                for cols in HALVES if t == 0 else (slice(0, S),):
+                    acc = bank("%s_acc%d_%d" % (name, t, cols.start), t, [P, cols.stop - cols.start])
+                    nc.tensor.matmul_mx(
+                        out=acc[:],
+                        lhsT=pair[0][:, ms].bitcast(FP8X4),
+                        lhsT_scale=pair[1][:, ms],
+                        rhs=moving[0][:, cols].bitcast(FP8X4),
+                        rhs_scale=moving[1][:, cols],
+                        start=True,
+                        stop=True,
+                    )
+                    bias = last_bias[:, 0:1] if t == PACK - 1 else 0.0
+                    nc.scalar.activation(rows[t][:, cols], acc[:], SILU, bias=bias)
+            return rows
 
-        def product(acc, wq, t, codes, scales):
-            cols = slice((t % 2) * P, (t % 2 + 1) * P)
-            nc.tensor.matmul_mx(
-                out=acc,
-                lhsT=wq[t // 2][0][:, cols].bitcast(FP8X4),
-                lhsT_scale=wq[t // 2][1][:, cols],
-                rhs=codes[:].bitcast(FP8X4),
-                rhs_scale=scales[:],
-                start=True,
-                stop=True,
-            )
-
-        on_scalar, on_vector = nc.scalar.copy, nc.vector.tensor_copy
-
-        xs = tile("xs", [P, T], U8, "xs")
-        nc.vector.memset(xs[:].bitcast(I32), 0)
-        warm_in = [tile("warm_in%d" % n, [P, 16], F32, ("w1_raw0", "w1_raw1", "w3s_raw")[n]) for n in range(3)]
-        for n in range(3):
-            nc.vector.memset(warm_in[n][:], 0.0)
-        warm_out = tile("warm_out", [P, 16], F32, "w1_raw2")
-        zero = [tile("zero%d" % n, [P, 16], F32, "late%d" % n) for n in range(2)]
-        for n in range(2):
-            nc.vector.memset(zero[n][:], 0.0)
         offs_t = load_list("offs_t", offs)
         s1_t = load_list("s1_t", s1)
-        xw = tile("xw", [P, T], I32, "xw")
+        xw = tile("xw", [P, T], I32)
         nc.sync.dma_start(xw[:], x_words[0].rearrange("p c r -> p (c r)").bitcast(I32))
-        load_scales(nc.sync, xs, x_scales)
-        nc.scalar.activation(warm_out[:], warm_in[0][:], SILU, bias=warm_in[1][:, 0:1], scale=warm_in[2][:, 0:1])
-        w1_raw = [load_rows("w1_raw%d" % n, w1, c0, width, None) for n, (c0, width) in enumerate(W1_CHUNKS)]
+        xs = load_scales("xs", x_scales)
         s2_t = load_list("s2_t", s2)
+        zero_bias = []
+        for n, successor in enumerate(("w1_rows", "w3s")):
+            zeros = tile("zeros%d" % n, [P, 16], F32, successor)
+            nc.vector.memset(zeros[:], 0.0)
+            zero_bias.append(tile("zero_bias%d" % n, [P, 16], F32))
+            nc.scalar.activation(zero_bias[n][:], zeros[:], SILU)
+        w1_rows = tile("w1_rows", [P, len(HALVES), PACK, H // 2], F32)
+        for u, cols in enumerate(HALVES):
+            nc.sync.dma_start(w1_rows[:, u, :, :], w1.rearrange("(p j) c -> p j c", j=PACK)[:, :, cols])
+        w3s = load_scales("w3s", w3_scales)
 
-        w3s_raw = tile("w3s_raw", [P, N], U8)
-        nc.vector.memset(w3s_raw[:].bitcast(I32), 0)
-        load_scales(nc.sync, w3s_raw, w3_scales)
-
-        xq_scales = tile("xq_scales", [P, S], U8)
-        nc.vector.tensor_copy(xq_scales[:], xs[:].indirect(offs_t[:]))
-        xq = tile("xq", [P, S], U32)
-        nc.vector.tensor_copy(xq[:], xw[:].bitcast(U32).indirect(offs_t[:]))
-
-        w2_raw = [load_rows("w2_raw0", w2, 0, 256, "xw")]
-
+        xq = packed("xq", S)
+        nc.vector.tensor_copy(xq[1][:], xs[:].indirect(offs_t[:]))
+        nc.vector.tensor_copy(xq[0][:], xw[:].bitcast(U32).indirect(offs_t[:]))
+        w2_rows = load_rows("w2_rows", w2, "xw")
         w1_bf = [tile("w1_bf%d" % u, [P, 2, P, PACK], BF16) for u in range(2)]
-        for raw, (c0, width) in zip(w1_raw, W1_CHUNKS):
-            round_weight(on_scalar, w1_bf[0], raw, c0, width, 0, 2)
-            round_weight(on_vector, w1_bf[1], raw, c0, width, 2, 4)
-        w1_q = [quantize("w1q%d" % u, w1_bf[u][:].rearrange("p t m j -> p (t m j)"), 2 * P, (None, "w1_bf0")[u]) for u in range(2)]
+        for u in range(len(HALVES)):
+            ms = slice(u * P // 2, (u + 1) * P // 2)
+            deal_weight(on_scalar, w1_bf[0][:, :, ms, :], w1_rows[:, u, :, :], slice(0, 2))
+            deal_weight(on_vector, w1_bf[1][:, :, ms, :], w1_rows[:, u, :, :], slice(2, 4))
+        w1_q = [packed("w1q0", 2 * P), packed("w1q1", 2 * P, "w1_bf0")]
+        for u in range(2):
+            quantize(w1_q[u], slice(0, 2 * P), w1_bf[u][:].rearrange("p t m j -> p (t m j)"))
+        y = hidden_layer("y", w1_q, xq, zero_bias[0])
 
-        w2_raw.append(load_rows("w2_raw1", w2, 256, 256, "w1_raw0"))
+        w3_rows = tile("w3_rows", [P, 2 * N], U8, "w1q0_codes")
+        nc.sync.dma_start(w3_rows[:].bitcast(I32), w3_words[0].bitcast(I32))
+        res_rows = load_rows("res_rows", res, "xq_codes")
+        w3_dealt_scales = tile("w3_dealt_scales", [P, PACK, P], U8, "w1_bf1")
+        nc.vector.tensor_copy(
+            w3_dealt_scales[:].rearrange("p t m -> p m t"), w3s[:].rearrange("p (m t) -> p m t", t=PACK)
+        )
 
-        y = [tile("y%d" % t, [P, S], F32) for t in range(PACK)]
-        for t in range(PACK):
-            acc = bank("acc1_%d" % t, t, [P, S])
-            product(acc[:], w1_q, t, xq, xq_scales)
-            nc.scalar.activation(y[t][:], acc[:], SILU, bias=zero[0][:, 0:1] if t == PACK - 1 else 0.0)
-
-        w3_raw = tile("w3_raw", [P, 2 * N], U8, "w1q0_codes")
-        nc.sync.dma_start(w3_raw[:].bitcast(I32), w3_words[0].bitcast(I32))
-        res_t = load_rows("res_t", res, 0, S, "xq")
-        w3_sc = tile("w3_sc", [P, PACK, P], U8, "w1_bf1")
-        nc.vector.tensor_copy(w3_sc[:].rearrange("p t m -> p m t"), w3s_raw[:].rearrange("p (m t) -> p m t", t=PACK))
-
-        z_planes = shuffle("z", y, s1_t, Z_CHUNKS[0:1]) + shuffle("z", y, s1_t, Z_CHUNKS[1:2], "late0")
+        z = [shuffle("z0", y, s1_t, HALVES[0]), shuffle("z1", y, s1_t, HALVES[1], "zero_bias0")]
         w2_bf = tile("w2_bf", [P, PACK, P, PACK], BF16)
-        for raw, (c0, width) in zip(w2_raw, W2_CHUNKS):
-            round_weight(on_scalar, w2_bf, raw, c0, width, 0, 4)
-        w2_q = quantize_weight("w2q", w2_bf)
-        h = [tile("h%d" % t, [P, S], F32) for t in range(PACK)]
-        woven = tile("zw", [P, S, PACK], BF16, "w1_raw0")
-        weave(on_scalar, woven[:, 0:256, :], z_planes[0][:])
-        weave(on_vector, woven[:, 256:384, :], z_planes[1][:, :, 0:128])
-        weave(on_scalar, woven[:, 384:512, :], z_planes[1][:, :, 128:256])
-        zq, zq_scales = quantize("zq", woven[:].rearrange("p c t -> p (c t)"), S)
-        for t in range(PACK):
-            acc = bank("acc2_%d" % t, t, [P, S])
-            product(acc[:], w2_q, t, zq, zq_scales)
-            nc.scalar.activation(h[t][:], acc[:], SILU, bias=zero[1][:, 0:1] if t == PACK - 1 else 0.0)
+        deal_weight(on_scalar, w2_bf[:], w2_rows[:], slice(0, PACK))
+        w2_q = [packed("w2q%d" % u, 2 * P) for u in range(2)]
+        for u in range(2):
+            quantize(w2_q[u], slice(0, 2 * P), w2_bf[:, 2 * u : 2 * u + 2, :, :].rearrange("p t m j -> p (t m j)"))
+        z_woven = tile("z_woven", [P, S, PACK], BF16, "xw")
+        quarter = S // 4
+        weave(on_scalar, z_woven[:, HALVES[0], :], z[0][:])
+        weave(on_vector, z_woven[:, 2 * quarter : 3 * quarter, :], z[1][:, :, 0:quarter])
+        weave(on_scalar, z_woven[:, 3 * quarter : S, :], z[1][:, :, quarter : 2 * quarter])
+        zq = packed("zq", S)
+        for cols in HALVES:
+            quantize(zq, cols, flat(z_woven[:, cols, :]))
+        h = hidden_layer("h", w2_q, zq, zero_bias[1])
 
-        w3_codes = tile("w3_codes", [P, PACK, P, 2], U8, "w1_raw0")
-        nc.vector.tensor_copy(w3_codes[:].rearrange("p t m b -> p m t b"), w3_raw[:].rearrange("p (m t b) -> p m t b", t=PACK, b=2))
+        w3_dealt = tile("w3_dealt", [P, PACK, P, 2], U8, "xw")
+        nc.vector.tensor_copy(
+            w3_dealt[:].rearrange("p t m b -> p m t b"), w3_rows[:].rearrange("p (m t b) -> p m t b", t=PACK, b=2)
+        )
 
-        o_codes = tile("o_codes", [P, S], U32)
-        o_scales = tile("o_scales", [P, S], U8)
+        out_q = packed("out_q", S)
         out_rows = out_0.rearrange("(p t) c -> p t c", t=PACK)
         out_words = out_1[0].rearrange("p c r -> p (c r)").bitcast(I32)
-        stage = {}
-        used = [0]
+        z2_woven, sums, out_woven, banks_used = {}, {}, {}, []
 
-        def gather3(n):
-            planes = shuffle("z2_", h, s2_t, O_CHUNKS[n : n + 1], (None, "late1", "z2w0")[n])
-            stage[n] = interleave("z2w%d" % n, planes[0], O_CHUNKS[n][1])
+        def gather(n, after):
+            width = CHUNKS[n].stop - CHUNKS[n].start
+            planes = shuffle("z2_%d" % n, h, s2_t, CHUNKS[n], after)
+            z2_woven[n] = tile("z2_woven%d" % n, [P, width, PACK], BF16)
+            weave(on_scalar, z2_woven[n][:], planes[:])
 
-        def mult3(n):
-            c0, width = O_CHUNKS[n]
-            codes, scales = quantize("z2q%d" % c0, stage[n], width)
+        def multiply(n):
+            width = CHUNKS[n].stop - CHUNKS[n].start
+            z2q = packed("z2q%d" % n, width)
+            quantize(z2q, slice(0, width), flat(z2_woven[n][:]))
             per_bank = BANK // width
-            banks = []
+            sums[n] = []
             for t in range(PACK):
                 if t % per_bank == 0:
-                    banks.append(bank("acc3_%d_%d" % (n, t), len(used) - 1, [P, per_bank, width]))
-                    used.append(0)
+                    sums[n].append(bank("out_acc%d_%d" % (n, t), len(banks_used), [P, per_bank, width]))
+                    banks_used.append(n)
                 nc.tensor.matmul_mx(
-                    out=banks[-1][:, t % per_bank, :],
-                    lhsT=w3_codes[:, t, :, :].rearrange("p m b -> p (m b)").bitcast(FP4X4),
-                    lhsT_scale=w3_sc[:, t, :],
-                    rhs=codes[:].bitcast(FP8X4),
-                    rhs_scale=scales[:],
+                    out=sums[n][-1][:, t % per_bank, :],
+                    lhsT=w3_dealt[:, t, :, :].rearrange("p m b -> p (m b)").bitcast(FP4X4),
+                    lhsT_scale=w3_dealt_scales[:, t, :],
+                    rhs=z2q[0][:].bitcast(FP8X4),
+                    rhs_scale=z2q[1][:],
                     start=True,
                     stop=True,
                 )
-            stage[n] = banks
 
-        def add3(n):
-            c0, width = O_CHUNKS[n]
+        def add_residual(n):
+            width = CHUNKS[n].stop - CHUNKS[n].start
             per_bank = BANK // width
-            summed = tile("sum%d" % c0, [P, PACK, width], F32)
-            for b, acc in enumerate(stage[n]):
-                rows = slice(b * per_bank, (b + 1) * per_bank)
-                nc.vector.tensor_tensor(summed[:, rows, :], acc[:], res_t[:, rows, c0 : c0 + width], ADD)
-            nc.sync.dma_start(out_rows[:, :, c0 : c0 + width], summed[:])
-            stage[n] = interleave("ow%d" % c0, summed, width)
+            result = tile("result%d" % n, [P, PACK, width], F32)
+            for b, acc in enumerate(sums[n]):
+                ts = slice(b * per_bank, (b + 1) * per_bank)
+                nc.vector.tensor_tensor(result[:, ts, :], acc[:], res_rows[:, ts, CHUNKS[n]], ADD)
+            nc.sync.dma_start(out_rows[:, :, CHUNKS[n]], result[:])
+            out_woven[n] = tile("out_woven%d" % n, [P, width, PACK], BF16)
+            weave(on_scalar, out_woven[n][:], result[:])
 
-        def planes3(n):
-            c0, width = O_CHUNKS[n]
-            cols = slice(c0, c0 + width)
-            nc.vector.quantize_mx(out=o_codes[:, cols].bitcast(FP8X4), scales=o_scales[:, cols], in_=stage[n])
-            nc.sync.dma_start(out_words[:, cols], o_codes[:, cols].bitcast(I32))
+        def hand_on(n):
+            quantize(out_q, CHUNKS[n], flat(out_woven[n][:]))
+            nc.sync.dma_start(out_words[:, CHUNKS[n]], out_q[0][:, CHUNKS[n]].bitcast(I32))
 
-        gather3(0)
-        gather3(1)
-        mult3(0)
-        gather3(2)
-        mult3(1)
-        add3(0)
-        mult3(2)
-        add3(1)
-        add3(2)
-        for n in range(3):
-            planes3(n)
-        for q in range(4):
-            eng = nc.sync if q % 2 == 0 else nc.scalar
-            eng.dma_start(out_2[0, 4 * q : 4 * q + 4, :].bitcast(I32), o_scales[32 * q : 32 * q + 4, :].bitcast(I32))
+        gather(0, None)
+        gather(1, "zero_bias1")
+        multiply(0)
+        gather(2, "z2_woven0")
+        multiply(1)
+        add_residual(0)
+        multiply(2)
+        add_residual(1)
+        add_residual(2)
+        for n in range(len(CHUNKS)):
+            hand_on(n)
+        for q in range(P // QUADRANT):
+            queue = nc.sync if q % 2 == 0 else nc.scalar
+            live = out_q[1][QUADRANT * q : QUADRANT * q + PACK, :]
+            queue.dma_start(out_2[0, PACK * q : PACK * q + PACK, :].bitcast(I32), live.bitcast(I32))

@@ -20,7 +20,7 @@ P = 128
 PACK = 4
 GROUP = 16
 QUADRANT = 32
-BANK = 512
+PIECE = 128
 HALVES = (slice(0, S // 2), slice(S // 2, S))
 CHUNKS = (slice(0, 256), slice(256, 384), slice(384, 512))
 
@@ -164,7 +164,10 @@ def tile_picked_shuf3_silu_po_kernel(
         out_q = packed("out_q", S)
         out_rows = out_0.rearrange("(p t) c -> p t c", t=PACK)
         out_words = out_1[0].rearrange("p c r -> p (c r)").bitcast(I32)
-        z2_woven, sums, out_woven, banks_used = {}, {}, {}, []
+        z2_woven, sums, out_woven = {}, {}, {}
+
+        def pieces(n):
+            return range(CHUNKS[n].start, CHUNKS[n].stop, PIECE)
 
         def gather(n, after):
             width = CHUNKS[n].stop - CHUNKS[n].start
@@ -176,32 +179,28 @@ def tile_picked_shuf3_silu_po_kernel(
             width = CHUNKS[n].stop - CHUNKS[n].start
             z2q = packed("z2q%d" % n, width)
             quantize(z2q, slice(0, width), flat(z2_woven[n][:]))
-            per_bank = BANK // width
-            sums[n] = []
-            for t in range(PACK):
-                if t % per_bank == 0:
-                    sums[n].append(bank("out_acc%d_%d" % (n, t), len(banks_used), [P, per_bank, width]))
-                    banks_used.append(n)
-                nc.tensor.matmul_mx(
-                    out=sums[n][-1][:, t % per_bank, :],
-                    lhsT=w3_dealt[:, t, :, :].rearrange("p m b -> p (m b)").bitcast(FP4X4),
-                    lhsT_scale=w3_dealt_scales[:, t, :],
-                    rhs=z2q[0][:].bitcast(FP8X4),
-                    rhs_scale=z2q[1][:],
-                    start=True,
-                    stop=True,
-                )
+            for c0 in pieces(n):
+                local = slice(c0 - CHUNKS[n].start, c0 - CHUNKS[n].start + PIECE)
+                sums[c0] = bank("out_acc%d" % c0, c0 // PIECE, [P, PACK, PIECE])
+                for t in range(PACK):
+                    nc.tensor.matmul_mx(
+                        out=sums[c0][:, t, :],
+                        lhsT=w3_dealt[:, t, :, :].rearrange("p m b -> p (m b)").bitcast(FP4X4),
+                        lhsT_scale=w3_dealt_scales[:, t, :],
+                        rhs=z2q[0][:, local].bitcast(FP8X4),
+                        rhs_scale=z2q[1][:, local],
+                        start=True,
+                        stop=True,
+                    )
 
         def add_residual(n):
-            width = CHUNKS[n].stop - CHUNKS[n].start
-            per_bank = BANK // width
-            result = tile("result%d" % n, [P, PACK, width], F32)
-            for b, acc in enumerate(sums[n]):
-                ts = slice(b * per_bank, (b + 1) * per_bank)
-                nc.vector.tensor_tensor(result[:, ts, :], acc[:], res_rows[:, ts, CHUNKS[n]], ADD)
-            nc.sync.dma_start(out_rows[:, :, CHUNKS[n]], result[:])
-            out_woven[n] = tile("out_woven%d" % n, [P, width, PACK], BF16)
-            weave(on_scalar, out_woven[n][:], result[:])
+            out_woven[n] = tile("out_woven%d" % n, [P, CHUNKS[n].stop - CHUNKS[n].start, PACK], BF16)
+            for c0 in pieces(n):
+                local = slice(c0 - CHUNKS[n].start, c0 - CHUNKS[n].start + PIECE)
+                result = tile("result%d" % c0, [P, PACK, PIECE], F32)
+                nc.vector.tensor_tensor(result[:], sums[c0][:], res_rows[:, :, c0 : c0 + PIECE], ADD)
+                nc.sync.dma_start(out_rows[:, :, c0 : c0 + PIECE], result[:])
+                weave(on_scalar, out_woven[n][:, local, :], result[:])
 
         def hand_on(n):
             quantize(out_q, CHUNKS[n], flat(out_woven[n][:]))

@@ -53,12 +53,12 @@ def tile_picked_shuf3_silu_po_kernel(
             nc.sync.dma_start(rows[:], src.rearrange("(p j) c -> p j c", j=PACK))
             return rows
 
-        def load_scales(name, src):
-            planes = tile(name, [P, src.shape[2]], U8)
+        def load_scales(name, src, queue, after=None):
+            planes = tile(name, [P, src.shape[2]], U8, after)
             nc.vector.memset(planes[:].bitcast(I32), 0)
             for q in range(P // QUADRANT):
                 live = planes[QUADRANT * q : QUADRANT * q + PACK, :]
-                nc.sync.dma_start(live.bitcast(I32), src[0, PACK * q : PACK * q + PACK, :].bitcast(I32))
+                queue.dma_start(live.bitcast(I32), src[0, PACK * q : PACK * q + PACK, :].bitcast(I32))
             return planes
 
         def deal_weight(copy, dealt, rows, tiles):
@@ -70,11 +70,9 @@ def tile_picked_shuf3_silu_po_kernel(
         def quantize(operand, cols, values):
             nc.vector.quantize_mx(out=operand[0][:, cols].bitcast(FP8X4), scales=operand[1][:, cols], in_=values)
 
-        def shuffle(name, rows, lst, cols, after=None):
-            planes = tile(name, [P, PACK, cols.stop - cols.start], BF16, after)
+        def shuffle(planes, rows, lst, cols):
             for t in range(PACK):
                 nc.vector.tensor_copy(planes[:, t, :], rows[t][:].indirect(entries(lst, cols)))
-            return planes
 
         def weave(copy, woven, planes):
             copy(woven.rearrange("p (c i) t -> p c t i", i=4), planes.rearrange("p t (c i) -> p c t i", i=4))
@@ -85,138 +83,157 @@ def tile_picked_shuf3_silu_po_kernel(
         def hidden_layer(name, weights, moving, last_bias):
             rows = [tile("%s%d" % (name, t), [P, S], F32) for t in range(PACK)]
             for t in range(PACK):
-                pair, ms = weights[t // 2], slice((t % 2) * P, (t % 2 + 1) * P)
-                for cols in HALVES if t == 0 else (slice(0, S),):
-                    acc = bank("%s_acc%d_%d" % (name, t, cols.start), t, [P, cols.stop - cols.start])
+                parts = CHUNKS if t == 0 else HALVES
+                for u, cols in enumerate(parts):
+                    acc = bank("%s_acc%d_%d" % (name, t, u), t if u < 2 else PACK - 1, [P, cols.stop - cols.start])
                     nc.tensor.matmul_mx(
                         out=acc[:],
-                        lhsT=pair[0][:, ms].bitcast(FP8X4),
-                        lhsT_scale=pair[1][:, ms],
+                        lhsT=weights[t][0].bitcast(FP8X4),
+                        lhsT_scale=weights[t][1],
                         rhs=moving[0][:, cols].bitcast(FP8X4),
                         rhs_scale=moving[1][:, cols],
                         start=True,
                         stop=True,
                     )
-                    bias = last_bias[:, 0:1] if t == PACK - 1 else 0.0
+                    bias = last_bias[:, 0:1] if (t, u) == (PACK - 1, 1) else 0.0
                     nc.scalar.activation(rows[t][:, cols], acc[:], SILU, bias=bias)
             return rows
 
+        def stationary(first, rest):
+            return [(first[0][:], first[1][:])] + [
+                (rest[0][:, t * P : (t + 1) * P], rest[1][:, t * P : (t + 1) * P]) for t in range(PACK - 1)
+            ]
+
+        def dealt(pair, ts):
+            return pair[:, ts, :, :].rearrange("p t m j -> p (t m j)")
+
         offs_t = load_list("offs_t", offs)
-        s1_t = load_list("s1_t", s1)
         xw = tile("xw", [P, T], I32)
         nc.sync.dma_start(xw[:], x_words[0].rearrange("p c r -> p (c r)").bitcast(I32))
-        xs = load_scales("xs", x_scales)
+        xs = load_scales("xs", x_scales, nc.scalar)
+        s1_t = load_list("s1_t", s1)
         s2_t = load_list("s2_t", s2)
-        zero_bias = []
-        for n, successor in enumerate(("w1_rows", "w3s")):
-            zeros = tile("zeros%d" % n, [P, 16], F32, successor)
-            nc.vector.memset(zeros[:], 0.0)
-            zero_bias.append(tile("zero_bias%d" % n, [P, 16], F32))
-            nc.scalar.activation(zero_bias[n][:], zeros[:], SILU)
-        w1_rows = tile("w1_rows", [P, len(HALVES), PACK, H // 2], F32)
-        for u, cols in enumerate(HALVES):
-            nc.sync.dma_start(w1_rows[:, u, :, :], w1.rearrange("(p j) c -> p j c", j=PACK)[:, :, cols])
-        w3s = load_scales("w3s", w3_scales)
+        zeros = tile("zeros", [P, 16], F32, "w1_rows")
+        nc.vector.memset(zeros[:], 0.0)
+        zero_bias = [tile("zero_bias%d" % n, [P, 16], F32) for n in range(2)]
+        nc.vector.tensor_copy(zero_bias[1][:], zeros[:])
+        nc.scalar.activation(zero_bias[0][:], zero_bias[1][:], SILU)
+        w1_rows = load_rows("w1_rows", w1, None)
 
         xq = packed("xq", S)
         nc.vector.tensor_copy(xq[1][:], xs[:].indirect(offs_t[:]))
         nc.vector.tensor_copy(xq[0][:], xw[:].bitcast(U32).indirect(offs_t[:]))
         w2_rows = load_rows("w2_rows", w2, "xw")
+        w3s = load_scales("w3s", w3_scales, nc.sync, "xs")
         w1_bf = [tile("w1_bf%d" % u, [P, 2, P, PACK], BF16) for u in range(2)]
-        for u in range(len(HALVES)):
-            ms = slice(u * P // 2, (u + 1) * P // 2)
-            deal_weight(on_scalar, w1_bf[0][:, :, ms, :], w1_rows[:, u, :, :], slice(0, 2))
-            deal_weight(on_vector, w1_bf[1][:, :, ms, :], w1_rows[:, u, :, :], slice(2, 4))
-        w1_q = [packed("w1q0", 2 * P), packed("w1q1", 2 * P, "w1_bf0")]
-        for u in range(2):
-            quantize(w1_q[u], slice(0, 2 * P), w1_bf[u][:].rearrange("p t m j -> p (t m j)"))
-        y = hidden_layer("y", w1_q, xq, zero_bias[0])
+        deal_weight(on_vector, w1_bf[0][:], w1_rows[:], slice(0, 2))
+        deal_weight(on_scalar, w1_bf[1][:], w1_rows[:], slice(2, 4))
+        w1_first, w1_rest = packed("w1q0", P), packed("w1q1", 3 * P)
+        quantize(w1_first, slice(0, P), dealt(w1_bf[0], slice(0, 1)))
+        quantize(w1_rest, slice(0, P), dealt(w1_bf[0], slice(1, 2)))
+        quantize(w1_rest, slice(P, 3 * P), dealt(w1_bf[1], slice(0, 2)))
+        y = hidden_layer("y", stationary(w1_first, w1_rest), xq, zero_bias[0])
 
         w3_rows = tile("w3_rows", [P, 2 * N], U8, "w1q0_codes")
         nc.sync.dma_start(w3_rows[:].bitcast(I32), w3_words[0].bitcast(I32))
         res_rows = load_rows("res_rows", res, "xq_codes")
-        w3_dealt_scales = tile("w3_dealt_scales", [P, PACK, P], U8, "w1_bf1")
-        nc.vector.tensor_copy(
-            w3_dealt_scales[:].rearrange("p t m -> p m t"), w3s[:].rearrange("p (m t) -> p m t", t=PACK)
-        )
+        w3_dealt_scales = tile("w3_dealt_scales", [P, PACK, P], U8, "w1_bf0")
+        nc.vector.tensor_copy(w3_dealt_scales[:], w3s[:].rearrange("p (m t) -> p t m", t=PACK))
 
-        z = [shuffle("z0", y, s1_t, HALVES[0]), shuffle("z1", y, s1_t, HALVES[1], "zero_bias0")]
-        w2_bf = tile("w2_bf", [P, PACK, P, PACK], BF16)
-        deal_weight(on_scalar, w2_bf[:], w2_rows[:], slice(0, PACK))
-        w2_q = [packed("w2q%d" % u, 2 * P) for u in range(2)]
-        for u in range(2):
-            quantize(w2_q[u], slice(0, 2 * P), w2_bf[:, 2 * u : 2 * u + 2, :, :].rearrange("p t m j -> p (t m j)"))
-        z_woven = tile("z_woven", [P, S, PACK], BF16, "xw")
-        quarter = S // 4
-        weave(on_scalar, z_woven[:, HALVES[0], :], z[0][:])
-        weave(on_vector, z_woven[:, 2 * quarter : 3 * quarter, :], z[1][:, :, 0:quarter])
-        weave(on_scalar, z_woven[:, 3 * quarter : S, :], z[1][:, :, quarter : 2 * quarter])
+        z_first = tile("z_first", [P, PACK, S // 2], BF16)
+        z_later = tile("z_later", [P, 2, PACK, PIECE], BF16, "zero_bias0")
+        z = [z_first[:], z_later[:, 0, :, :], z_later[:, 1, :, :]]
+        for n, cols in enumerate(CHUNKS):
+            shuffle(z[n], y, s1_t, cols)
+        w2_bf = [tile("w2_bf%d" % u, [P, 2, P, PACK], BF16) for u in range(2)]
+        z_woven = [tile("z_woven%d" % n, [P, c.stop - c.start, PACK], BF16) for n, c in enumerate(CHUNKS)]
+        deal_weight(on_scalar, w2_bf[0][:], w2_rows[:], slice(0, 2))
+        weave(on_scalar, z_woven[0][:], z[0])
+        deal_weight(on_scalar, w2_bf[1][:], w2_rows[:], slice(2, 4))
+        weave(on_scalar, z_woven[1][:], z[1])
+        weave(on_scalar, z_woven[2][:], z[2])
+        w2_first, w2_rest = packed("w2q0", P), packed("w2q1", 3 * P, "zero_bias0")
         zq = packed("zq", S)
-        for cols in HALVES:
-            quantize(zq, cols, flat(z_woven[:, cols, :]))
-        h = hidden_layer("h", w2_q, zq, zero_bias[1])
+        quantize(w2_first, slice(0, P), dealt(w2_bf[0], slice(0, 1)))
+        for n, cols in enumerate(CHUNKS):
+            quantize(zq, cols, flat(z_woven[n][:]))
+        quantize(w2_rest, slice(0, P), dealt(w2_bf[0], slice(1, 2)))
+        quantize(w2_rest, slice(P, 3 * P), dealt(w2_bf[1], slice(0, 2)))
+        h = hidden_layer("h", stationary(w2_first, w2_rest), zq, zero_bias[1])
 
-        w3_dealt = tile("w3_dealt", [P, PACK, P, 2], U8, "xw")
-        nc.vector.tensor_copy(
-            w3_dealt[:].rearrange("p t m b -> p m t b"), w3_rows[:].rearrange("p (m t b) -> p m t b", t=PACK, b=2)
-        )
+        w3_dealt = tile("w3_dealt", [P, PACK, P, 2], U8, "z_woven2")
+        nc.vector.tensor_copy(w3_dealt[:], w3_rows[:].rearrange("p (m t b) -> p t m b", t=PACK, b=2))
 
         out_q = packed("out_q", S)
         out_rows = out_0.rearrange("(p t) c -> p t c", t=PACK)
         out_words = out_1[0].rearrange("p c r -> p (c r)").bitcast(I32)
-        z2_woven, sums, out_woven = {}, {}, {}
+        pieces = [slice(c0, c0 + PIECE) for c0 in range(0, S, PIECE)]
+        z2_planes = [
+            tile("z2_%d" % n, [P, PACK, cols.stop - cols.start], BF16, after)
+            for n, (cols, after) in enumerate(zip(CHUNKS[:2], (None, "zero_bias1")))
+        ]
+        z2_woven = [tile("z2_woven%d" % n, [P, PIECE, PACK], BF16) for n in range(len(pieces))]
+        out_woven = [tile("out_woven%d" % n, [P, c.stop - c.start, PACK], BF16) for n, c in enumerate(CHUNKS)]
+        out_pieces = [out_woven[0][:, 0:PIECE, :], out_woven[0][:, PIECE : 2 * PIECE, :], out_woven[1][:], out_woven[2][:]]
+        sums, results = {}, {}
 
-        def pieces(n):
-            return range(CHUNKS[n].start, CHUNKS[n].stop, PIECE)
-
-        def gather(n, after):
-            width = CHUNKS[n].stop - CHUNKS[n].start
-            planes = shuffle("z2_%d" % n, h, s2_t, CHUNKS[n], after)
-            z2_woven[n] = tile("z2_woven%d" % n, [P, width, PACK], BF16)
-            weave(on_scalar, z2_woven[n][:], planes[:])
+        def plane_groups(n):
+            return (slice(0, 2), slice(2, 4)) if n == len(pieces) - 1 else (slice(0, PACK),)
 
         def multiply(n):
-            width = CHUNKS[n].stop - CHUNKS[n].start
-            z2q = packed("z2q%d" % n, width)
-            quantize(z2q, slice(0, width), flat(z2_woven[n][:]))
-            for c0 in pieces(n):
-                local = slice(c0 - CHUNKS[n].start, c0 - CHUNKS[n].start + PIECE)
-                sums[c0] = bank("out_acc%d" % c0, c0 // PIECE, [P, PACK, PIECE])
-                for t in range(PACK):
+            z2q = packed("z2q%d" % n, PIECE)
+            quantize(z2q, slice(0, PIECE), flat(z2_woven[n][:]))
+            sums[n] = []
+            for planes in plane_groups(n):
+                acc = bank("out_acc%d_%d" % (n, planes.start), (n + planes.start) % PACK, [P, planes.stop - planes.start, PIECE])
+                sums[n].append(acc)
+                for t in range(planes.start, planes.stop):
                     nc.tensor.matmul_mx(
-                        out=sums[c0][:, t, :],
+                        out=acc[:, t - planes.start, :],
                         lhsT=w3_dealt[:, t, :, :].rearrange("p m b -> p (m b)").bitcast(FP4X4),
                         lhsT_scale=w3_dealt_scales[:, t, :],
-                        rhs=z2q[0][:, local].bitcast(FP8X4),
-                        rhs_scale=z2q[1][:, local],
+                        rhs=z2q[0][:].bitcast(FP8X4),
+                        rhs_scale=z2q[1][:],
                         start=True,
                         stop=True,
                     )
 
         def add_residual(n):
-            out_woven[n] = tile("out_woven%d" % n, [P, CHUNKS[n].stop - CHUNKS[n].start, PACK], BF16)
-            for c0 in pieces(n):
-                local = slice(c0 - CHUNKS[n].start, c0 - CHUNKS[n].start + PIECE)
-                result = tile("result%d" % c0, [P, PACK, PIECE], F32)
-                nc.vector.tensor_tensor(result[:], sums[c0][:], res_rows[:, :, c0 : c0 + PIECE], ADD)
-                nc.sync.dma_start(out_rows[:, :, c0 : c0 + PIECE], result[:])
-                weave(on_scalar, out_woven[n][:, local, :], result[:])
+            results[n] = tile("result%d" % n, [P, PACK, PIECE], F32)
+            for planes, acc in zip(plane_groups(n), sums[n]):
+                nc.vector.tensor_tensor(results[n][:, planes, :], acc[:], res_rows[:, planes, pieces[n]], ADD)
+            nc.sync.dma_start(out_rows[:, :, pieces[n]], results[n][:])
 
         def hand_on(n):
             quantize(out_q, CHUNKS[n], flat(out_woven[n][:]))
-            nc.sync.dma_start(out_words[:, CHUNKS[n]], out_q[0][:, CHUNKS[n]].bitcast(I32))
 
-        gather(0, None)
-        gather(1, "zero_bias1")
+        def store_words(cols):
+            nc.sync.dma_start(out_words[:, cols], out_q[0][:, cols].bitcast(I32))
+
+        for n in range(2):
+            shuffle(z2_planes[n][:], h, s2_t, CHUNKS[n])
+        for n in range(2):
+            weave(on_scalar, z2_woven[n][:], z2_planes[0][:, :, pieces[n]])
         multiply(0)
-        gather(2, "z2_woven0")
         multiply(1)
-        add_residual(0)
+        z2_last = tile("z2_2", [P, PACK, PIECE], BF16, "z2_0")
+        shuffle(z2_last[:], h, s2_t, CHUNKS[2])
+        weave(on_scalar, z2_woven[2][:], z2_planes[1][:])
+        weave(on_scalar, z2_woven[3][:], z2_last[:])
         multiply(2)
-        add_residual(1)
-        add_residual(2)
-        for n in range(len(CHUNKS)):
-            hand_on(n)
+        add_residual(0)
+        multiply(3)
+        for n in range(1, len(pieces)):
+            add_residual(n)
+        for n in range(len(pieces) - 1):
+            weave(on_scalar, out_pieces[n], results[n][:])
+        hand_on(0)
+        store_words(HALVES[0])
+        weave(on_vector, out_pieces[3][:, 0 : PIECE // 2, :], results[3][:, :, 0 : PIECE // 2])
+        weave(on_scalar, out_pieces[3][:, PIECE // 2 : PIECE, :], results[3][:, :, PIECE // 2 : PIECE])
+        hand_on(1)
+        hand_on(2)
+        store_words(HALVES[1])
         for q in range(P // QUADRANT):
             queue = nc.sync if q % 2 == 0 else nc.scalar
             live = out_q[1][QUADRANT * q : QUADRANT * q + PACK, :]

@@ -100,7 +100,7 @@ def tile_picked_shuf3_silu_po_kernel(
             return rows
 
         def stationary(first, rest):
-            return [(first[0][:], first[1][:])] + [
+            return [(first[0][:, 0:P], first[1][:, 0:P])] + [
                 (rest[0][:, t * P : (t + 1) * P], rest[1][:, t * P : (t + 1) * P]) for t in range(PACK - 1)
             ]
 
@@ -108,36 +108,37 @@ def tile_picked_shuf3_silu_po_kernel(
             return pair[:, ts, :, :].rearrange("p t m j -> p (t m j)")
 
         offs_t = load_list("offs_t", offs)
-        xw = tile("xw", [P, T], I32)
-        nc.sync.dma_start(xw[:], x_words[0].rearrange("p c r -> p (c r)").bitcast(I32))
+        w1_rows = load_rows("w1_rows", w1, None)
         xs = load_scales("xs", x_scales, nc.scalar)
         s1_t = load_list("s1_t", s1)
         s2_t = load_list("s2_t", s2)
-        zeros = tile("zeros", [P, 16], F32, "w1_rows")
+        zeros = tile("zeros", [P, 16], F32, "xw")
         nc.vector.memset(zeros[:], 0.0)
         zero_bias = [tile("zero_bias%d" % n, [P, 16], F32) for n in range(2)]
         nc.vector.tensor_copy(zero_bias[1][:], zeros[:])
         nc.scalar.activation(zero_bias[0][:], zero_bias[1][:], SILU)
-        w1_rows = load_rows("w1_rows", w1, None)
+        xw = tile("xw", [P, T], I32)
+        nc.sync.dma_start(xw[:], x_words[0].rearrange("p c r -> p (c r)").bitcast(I32))
 
-        xq = packed("xq", S)
-        nc.vector.tensor_copy(xq[1][:], xs[:].indirect(offs_t[:]))
-        nc.vector.tensor_copy(xq[0][:], xw[:].bitcast(U32).indirect(offs_t[:]))
-        w2_rows = load_rows("w2_rows", w2, "xw")
-        w3s = load_scales("w3s", w3_scales, nc.sync, "xs")
         w1_bf = [tile("w1_bf%d" % u, [P, 2, P, PACK], BF16) for u in range(2)]
         deal_weight(on_vector, w1_bf[0][:], w1_rows[:], slice(0, 2))
         deal_weight(on_scalar, w1_bf[1][:], w1_rows[:], slice(2, 4))
-        w1_first, w1_rest = packed("w1q0", P), packed("w1q1", 3 * P)
-        quantize(w1_first, slice(0, P), dealt(w1_bf[0], slice(0, 1)))
-        quantize(w1_rest, slice(0, P), dealt(w1_bf[0], slice(1, 2)))
-        quantize(w1_rest, slice(P, 3 * P), dealt(w1_bf[1], slice(0, 2)))
+        w2_rows = load_rows("w2_rows", w2, "w1_rows")
+        xq = packed("xq", S)
+        nc.vector.tensor_copy(xq[1][:], xs[:].indirect(offs_t[:]))
+        w3s = load_scales("w3s", w3_scales, nc.sync, "xs")
+        w1_q = packed("w1q0", PACK * P)
+        for u in range(2):
+            quantize(w1_q, slice(2 * u * P, 2 * (u + 1) * P), dealt(w1_bf[u], slice(0, 2)))
+        w1_first, w1_rest = (w1_q[0][:, 0:P], w1_q[1][:, 0:P]), (w1_q[0][:, P:], w1_q[1][:, P:])
+        for cols in HALVES:
+            nc.vector.tensor_copy(xq[0][:, cols], xw[:].bitcast(U32).indirect(entries(offs_t, cols)))
         y = hidden_layer("y", stationary(w1_first, w1_rest), xq, zero_bias[0])
 
         w3_rows = tile("w3_rows", [P, 2 * N], U8, "w1q0_codes")
         nc.sync.dma_start(w3_rows[:].bitcast(I32), w3_words[0].bitcast(I32))
         res_rows = load_rows("res_rows", res, "xq_codes")
-        w3_dealt_scales = tile("w3_dealt_scales", [P, PACK, P], U8, "w1_bf0")
+        w3_dealt_scales = tile("w3_dealt_scales", [P, PACK, P], U8, "xw")
         nc.vector.tensor_copy(w3_dealt_scales[:], w3s[:].rearrange("p (m t) -> p t m", t=PACK))
 
         z_first = tile("z_first", [P, PACK, S // 2], BF16)

@@ -32,9 +32,12 @@ def tile_picked_shuf3_silu_po_kernel(
     on_scalar, on_vector = nc.scalar.copy, nc.vector.tensor_copy
     with ExitStack() as ctx:
         keep = ctx.enter_context(tc.tile_pool(name="keep", bufs=1))
+        placed = ctx.enter_context(tc.tile_pool(name="placed", bufs=1))
         psum = ctx.enter_context(tc.psum_pool(name="psum", bufs=2))
 
         def tile(name, shape, dtype, after=None):
+            if isinstance(after, int):
+                return placed.tile(shape, dtype, name=name, offset=after, align_bytes=64)
             return keep.tile(shape, dtype, name=name, tag=after or name, align_bytes=64)
 
         def bank(name, tag, shape):
@@ -80,7 +83,7 @@ def tile_picked_shuf3_silu_po_kernel(
         def flat(woven):
             return woven.rearrange("p c t -> p (c t)")
 
-        def hidden_layer(name, weights, moving, last_bias):
+        def hidden_layer(name, weights, moving, last_bias, last_scale):
             rows = [tile("%s%d" % (name, t), [P, S], F32) for t in range(PACK)]
             for t in range(PACK):
                 parts = CHUNKS if t == 0 else HALVES
@@ -95,8 +98,9 @@ def tile_picked_shuf3_silu_po_kernel(
                         start=True,
                         stop=True,
                     )
-                    bias = last_bias[:, 0:1] if (t, u) == (PACK - 1, 1) else 0.0
-                    nc.scalar.activation(rows[t][:, cols], acc[:], SILU, bias=bias)
+                    last = (t, u) == (PACK - 1, 1)
+                    bias, scale = (last_bias, last_scale) if last else (0.0, 1.0)
+                    nc.scalar.activation(rows[t][:, cols], acc[:], SILU, bias=bias, scale=scale)
             return rows
 
         def stationary(first, rest):
@@ -112,58 +116,68 @@ def tile_picked_shuf3_silu_po_kernel(
         xs = load_scales("xs", x_scales, nc.scalar)
         s1_t = load_list("s1_t", s1)
         s2_t = load_list("s2_t", s2)
-        zeros = tile("zeros", [P, 16], F32, "xw")
+        zeros = tile("zeros", [P, 32], F32, 4 * T - 64)
         nc.vector.memset(zeros[:], 0.0)
         zero_bias = [tile("zero_bias%d" % n, [P, 16], F32) for n in range(2)]
-        nc.vector.tensor_copy(zero_bias[1][:], zeros[:])
-        nc.scalar.activation(zero_bias[0][:], zero_bias[1][:], SILU)
-        xw = tile("xw", [P, T], I32)
+        nc.vector.tensor_copy(zero_bias[1][:], zeros[:, 8:24])
+        nc.vector.memset(zero_bias[0][:], 1.0)
+        w2_bf = tile("w2_bf", [P, PACK, P, PACK], BF16)
+        nc.scalar.activation(w2_bf[:, 0, P // 2, :], zero_bias[1][:, 0:PACK], SILU)
+        xw = tile("xw", [P, T], I32, 0)
         nc.sync.dma_start(xw[:], x_words[0].rearrange("p c r -> p (c r)").bitcast(I32))
 
         w1_bf = [tile("w1_bf%d" % u, [P, 2, P, PACK], BF16) for u in range(2)]
         deal_weight(on_vector, w1_bf[0][:], w1_rows[:], slice(0, 2))
         deal_weight(on_scalar, w1_bf[1][:], w1_rows[:], slice(2, 4))
-        w2_rows = load_rows("w2_rows", w2, "w1_rows")
+        w2_left = load_rows("w2_left", w2[:, 0 : H // 2], 4 * T)
         xq = packed("xq", S)
         nc.vector.tensor_copy(xq[1][:], xs[:].indirect(offs_t[:]))
         w3s = load_scales("w3s", w3_scales, nc.sync, "xs")
         w1_q = packed("w1q0", PACK * P)
         for u in range(2):
             quantize(w1_q, slice(2 * u * P, 2 * (u + 1) * P), dealt(w1_bf[u], slice(0, 2)))
+        w2_right = load_rows("w2_right", w2[:, H // 2 : H], "w1_bf0")
         w1_first, w1_rest = (w1_q[0][:, 0:P], w1_q[1][:, 0:P]), (w1_q[0][:, P:], w1_q[1][:, P:])
         for cols in HALVES:
             nc.vector.tensor_copy(xq[0][:, cols], xw[:].bitcast(U32).indirect(entries(offs_t, cols)))
-        y = hidden_layer("y", stationary(w1_first, w1_rest), xq, zero_bias[0])
+        for ts in (slice(0, 2), slice(2, 4)):
+            deal_weight(on_vector, w2_bf[:, ts, 0 : P // 2, :], w2_left[:], ts)
+        y = hidden_layer("y", stationary(w1_first, w1_rest), xq, w2_bf[:, 0, P // 2, 0:1], zero_bias[0][:, 0:1])
 
         w3_rows = tile("w3_rows", [P, 2 * N], U8, "w1q0_codes")
         nc.sync.dma_start(w3_rows[:].bitcast(I32), w3_words[0].bitcast(I32))
         res_rows = load_rows("res_rows", res, "xq_codes")
-        w3_dealt_scales = tile("w3_dealt_scales", [P, PACK, P], U8, "xw")
-        nc.vector.tensor_copy(w3_dealt_scales[:], w3s[:].rearrange("p (m t) -> p t m", t=PACK))
 
-        z_first = tile("z_first", [P, PACK, S // 2], BF16)
-        z_later = tile("z_later", [P, 2, PACK, PIECE], BF16, "zero_bias0")
-        z = [z_first[:], z_later[:, 0, :, :], z_later[:, 1, :, :]]
-        for n, cols in enumerate(CHUNKS):
-            shuffle(z[n], y, s1_t, cols)
-        w2_bf = [tile("w2_bf%d" % u, [P, 2, P, PACK], BF16) for u in range(2)]
-        z_woven = [tile("z_woven%d" % n, [P, c.stop - c.start, PACK], BF16) for n, c in enumerate(CHUNKS)]
-        deal_weight(on_scalar, w2_bf[0][:], w2_rows[:], slice(0, 2))
-        weave(on_scalar, z_woven[0][:], z[0])
-        deal_weight(on_scalar, w2_bf[1][:], w2_rows[:], slice(2, 4))
-        weave(on_scalar, z_woven[1][:], z[1])
-        weave(on_scalar, z_woven[2][:], z[2])
+        z_first = tile("z_first", [P, PACK, S // 2], BF16, 4 * T)
+        z_later = tile("z_later", [P, PACK, S // 2], BF16, "zero_bias0")
+        shuffle(z_first[:], y, s1_t, HALVES[0])
+        for t in range(2):
+            nc.vector.tensor_copy(z_later[:, t, :], y[t][:].indirect(entries(s1_t, HALVES[1])))
+        for n, cols in enumerate(CHUNKS[1:]):
+            for t in range(2, PACK):
+                nc.vector.tensor_copy(z_later[:, t, n * PIECE : (n + 1) * PIECE], y[t][:].indirect(entries(s1_t, cols)))
+        z = [z_first[:], z_later[:, :, 0:PIECE], z_later[:, :, PIECE : 2 * PIECE]]
+        z_woven = [tile("z_woven%d" % n, [P, c.stop - c.start, PACK], BF16, ("w1_bf0", 4 * T, 4 * T + 1024)[n]) for n, c in enumerate(CHUNKS)]
+        for ts in (slice(0, 2), slice(2, 4)):
+            deal_weight(on_scalar, w2_bf[:, ts, P // 2 : P, :], w2_right[:], ts)
+        for n in range(len(CHUNKS)):
+            weave(on_scalar, z_woven[n][:], z[n])
         w2_first, w2_rest = packed("w2q0", P), packed("w2q1", 3 * P, "zero_bias0")
         zq = packed("zq", S)
-        quantize(w2_first, slice(0, P), dealt(w2_bf[0], slice(0, 1)))
+        quantize(w2_first, slice(0, P), dealt(w2_bf, slice(0, 1)))
         for n, cols in enumerate(CHUNKS):
             quantize(zq, cols, flat(z_woven[n][:]))
-        quantize(w2_rest, slice(0, P), dealt(w2_bf[0], slice(1, 2)))
-        quantize(w2_rest, slice(P, 3 * P), dealt(w2_bf[1], slice(0, 2)))
-        h = hidden_layer("h", stationary(w2_first, w2_rest), zq, zero_bias[1])
+        quantize(w2_rest, slice(0, P), dealt(w2_bf, slice(1, 2)))
+        quantize(w2_rest, slice(P, 3 * P), dealt(w2_bf, slice(2, 4)))
+        h = hidden_layer("h", stationary(w2_first, w2_rest), zq, zero_bias[1][:, 0:1], 1.0)
 
-        w3_dealt = tile("w3_dealt", [P, PACK, P, 2], U8, "z_woven2")
-        nc.vector.tensor_copy(w3_dealt[:], w3_rows[:].rearrange("p (m t b) -> p t m b", t=PACK, b=2))
+        w3_dealt_scales = tile("w3_dealt_scales", [P, PACK, P], U8, 4 * T + 1024)
+        nc.vector.tensor_copy(w3_dealt_scales[:], w3s[:].rearrange("p (m t) -> p t m", t=PACK))
+        w3_dealt = tile("w3_dealt", [P, PACK, P, 2], U8, 4 * T + 1536)
+        nc.vector.tensor_copy(
+            w3_dealt[:].rearrange("p t m b -> p (t m b)").bitcast(U16).rearrange("p (t m) -> p t m", t=PACK),
+            w3_rows[:].bitcast(U16).rearrange("p (m t) -> p t m", t=PACK),
+        )
 
         out_q = packed("out_q", S)
         out_rows = out_0.rearrange("(p t) c -> p t c", t=PACK)

@@ -78,7 +78,7 @@ def tile_picked_shuf3_silu_po_kernel(
                 nc.vector.tensor_copy(planes[:, t, :], rows[t][:].indirect(entries(lst, cols)))
 
         def weave(copy, woven, planes):
-            copy(woven.rearrange("p (c i) t -> p c t i", i=4), planes.rearrange("p t (c i) -> p c t i", i=4))
+            copy(woven.rearrange("p (c i) t -> p c t i", i=2), planes.rearrange("p t (c i) -> p c t i", i=2))
 
         def flat(woven):
             return woven.rearrange("p c t -> p (c t)")

@@ -14,7 +14,10 @@ U8 = mybir.dt.uint8
 FP8X4 = mybir.dt.float8_e4m3fn_x4
 FP4X4 = mybir.dt.float4_e2m1fn_x4
 SILU = mybir.ActivationFunctionType.Silu
+COPY = mybir.ActivationFunctionType.Copy
 ADD = mybir.AluOpType.add
+MULT = mybir.AluOpType.mult
+ALONG_ROW = mybir.AxisListType.X
 
 P = 128
 PACK = 4
@@ -23,6 +26,10 @@ QUADRANT = 32
 PIECE = 128
 HALVES = (slice(0, S // 2), slice(S // 2, S))
 CHUNKS = (slice(0, 256), slice(256, 384), slice(384, 512))
+PICKS = (slice(0, 128), slice(128, 384), slice(384, 512))
+RUN = 4
+STAGE = 4 * T
+WOVEN = 2 * PACK * PIECE
 
 
 def tile_picked_shuf3_silu_po_kernel(
@@ -33,15 +40,18 @@ def tile_picked_shuf3_silu_po_kernel(
     with ExitStack() as ctx:
         keep = ctx.enter_context(tc.tile_pool(name="keep", bufs=1))
         placed = ctx.enter_context(tc.tile_pool(name="placed", bufs=1))
-        psum = ctx.enter_context(tc.psum_pool(name="psum", bufs=2))
+        psum = ctx.enter_context(tc.psum_pool(name="psum", bufs=1))
 
         def tile(name, shape, dtype, after=None):
             if isinstance(after, int):
                 return placed.tile(shape, dtype, name=name, offset=after, align_bytes=64)
             return keep.tile(shape, dtype, name=name, tag=after or name, align_bytes=64)
 
-        def bank(name, tag, shape):
-            return psum.tile(shape, F32, name=name, tag="bank%d" % tag)
+        banks_taken = []
+
+        def bank(name, shape):
+            banks_taken.append(name)
+            return psum.tile(shape, F32, name=name, tag="bank%d" % (len(banks_taken) % 8))
 
         def entries(lst, cols):
             return lst[:, cols.start // GROUP : cols.stop // GROUP]
@@ -73,24 +83,31 @@ def tile_picked_shuf3_silu_po_kernel(
         def quantize(operand, cols, values):
             nc.vector.quantize_mx(out=operand[0][:, cols].bitcast(FP8X4), scales=operand[1][:, cols], in_=values)
 
-        def shuffle(planes, rows, lst, cols):
+        def gather_on_vector(plane, row, lst, cols):
+            nc.vector.tensor_copy(plane, row[:].indirect(entries(lst, cols)))
+
+        def gather_on_scalar(plane, row, lst, cols):
+            nc.scalar.activation(plane, row[:].indirect(entries(lst, cols)), COPY)
+
+        def shuffle(planes, rows, lst, cols, vector_planes):
             for t in range(PACK):
-                nc.vector.tensor_copy(planes[:, t, :], rows[t][:].indirect(entries(lst, cols)))
+                gather = gather_on_vector if t < vector_planes else gather_on_scalar
+                gather(planes[:, t, :], rows[t], lst, cols)
 
         def weave(copy, woven, planes):
-            copy(woven.rearrange("p (c i) t -> p c t i", i=2), planes.rearrange("p t (c i) -> p c t i", i=2))
+            copy(woven.rearrange("p (c i) t -> p c t i", i=RUN), planes.rearrange("p t (c i) -> p c t i", i=RUN))
 
         def flat(woven):
             return woven.rearrange("p c t -> p (c t)")
 
-        def hidden_layer(name, weights, moving, last_bias, last_scale):
+        def hidden_layer(name, weights, moving, steps, last_bias):
             rows = [tile("%s%d" % (name, t), [P, S], F32) for t in range(PACK)]
-            for t in range(PACK):
-                parts = CHUNKS if t == 0 else HALVES
-                for u, cols in enumerate(parts):
-                    acc = bank("%s_acc%d_%d" % (name, t, u), t if u < 2 else PACK - 1, [P, cols.stop - cols.start])
+            for n, (t, chunks) in enumerate(steps):
+                first, end = chunks[0].start, chunks[-1].stop
+                acc = bank("%s_acc%d" % (name, n), [P, end - first])
+                for cols in chunks:
                     nc.tensor.matmul_mx(
-                        out=acc[:],
+                        out=acc[:, cols.start - first : cols.stop - first],
                         lhsT=weights[t][0].bitcast(FP8X4),
                         lhsT_scale=weights[t][1],
                         rhs=moving[0][:, cols].bitcast(FP8X4),
@@ -98,15 +115,12 @@ def tile_picked_shuf3_silu_po_kernel(
                         start=True,
                         stop=True,
                     )
-                    last = (t, u) == (PACK - 1, 1)
-                    bias, scale = (last_bias, last_scale) if last else (0.0, 1.0)
-                    nc.scalar.activation(rows[t][:, cols], acc[:], SILU, bias=bias, scale=scale)
+                bias = last_bias[:] if n == len(steps) - 1 else 0.0
+                nc.scalar.activation(rows[t][:, first:end], acc[:], SILU, bias=bias)
             return rows
 
-        def stationary(first, rest):
-            return [(first[0][:, 0:P], first[1][:, 0:P])] + [
-                (rest[0][:, t * P : (t + 1) * P], rest[1][:, t * P : (t + 1) * P]) for t in range(PACK - 1)
-            ]
+        def stationary(operand, count):
+            return [(operand[0][:, t * P : (t + 1) * P], operand[1][:, t * P : (t + 1) * P]) for t in range(count)]
 
         def dealt(pair, ts):
             return pair[:, ts, :, :].rearrange("p t m j -> p (t m j)")
@@ -116,64 +130,70 @@ def tile_picked_shuf3_silu_po_kernel(
         xs = load_scales("xs", x_scales, nc.scalar)
         s1_t = load_list("s1_t", s1)
         s2_t = load_list("s2_t", s2)
-        zeros = tile("zeros", [P, 32], F32, 4 * T - 64)
+        zeros = tile("zeros", [P, 2, GROUP], F32, STAGE - 4 * GROUP)
         nc.vector.memset(zeros[:], 0.0)
-        zero_bias = [tile("zero_bias%d" % n, [P, 16], F32) for n in range(2)]
-        nc.vector.tensor_copy(zero_bias[1][:], zeros[:, 8:24])
-        nc.vector.memset(zero_bias[0][:], 1.0)
-        w2_bf = tile("w2_bf", [P, PACK, P, PACK], BF16)
-        nc.scalar.activation(w2_bf[:, 0, P // 2, :], zero_bias[1][:, 0:PACK], SILU)
+        y_bias, h_bias = tile("y_bias", [P, 1], F32), tile("h_bias", [P, 1], F32)
+        nc.vector.tensor_reduce(y_bias[:], zeros[:, 0, :], ALONG_ROW, ADD)
+        nc.vector.tensor_reduce(h_bias[:], zeros[:, 1, :], ALONG_ROW, ADD)
         xw = tile("xw", [P, T], I32, 0)
         nc.sync.dma_start(xw[:], x_words[0].rearrange("p c r -> p (c r)").bitcast(I32))
 
         w1_bf = [tile("w1_bf%d" % u, [P, 2, P, PACK], BF16) for u in range(2)]
         deal_weight(on_vector, w1_bf[0][:], w1_rows[:], slice(0, 2))
         deal_weight(on_scalar, w1_bf[1][:], w1_rows[:], slice(2, 4))
-        w2_left = load_rows("w2_left", w2[:, 0 : H // 2], 4 * T)
+        w2_left = load_rows("w2_left", w2[:, 0 : H // 2], STAGE)
         xq = packed("xq", S)
         nc.vector.tensor_copy(xq[1][:], xs[:].indirect(offs_t[:]))
-        w3s = load_scales("w3s", w3_scales, nc.sync, "xs")
-        w1_q = packed("w1q0", PACK * P)
+        w1_q = packed("w1q", PACK * P)
         for u in range(2):
             quantize(w1_q, slice(2 * u * P, 2 * (u + 1) * P), dealt(w1_bf[u], slice(0, 2)))
         w2_right = load_rows("w2_right", w2[:, H // 2 : H], "w1_bf0")
-        w1_first, w1_rest = (w1_q[0][:, 0:P], w1_q[1][:, 0:P]), (w1_q[0][:, P:], w1_q[1][:, P:])
-        for cols in HALVES:
+        for cols in PICKS:
             nc.vector.tensor_copy(xq[0][:, cols], xw[:].bitcast(U32).indirect(entries(offs_t, cols)))
+        w3s = load_scales("w3s", w3_scales, nc.sync, 0)
+        w2_bf = tile("w2_bf", [P, PACK, P, PACK], BF16)
         for ts in (slice(0, 2), slice(2, 4)):
             deal_weight(on_vector, w2_bf[:, ts, 0 : P // 2, :], w2_left[:], ts)
-        y = hidden_layer("y", stationary(w1_first, w1_rest), xq, w2_bf[:, 0, P // 2, 0:1], zero_bias[0][:, 0:1])
+        steps = [(t, PICKS[0:1]) for t in range(PACK)] + [(0, PICKS[1:2]), (0, PICKS[2:3])]
+        steps = steps + [(t, PICKS[1:3]) for t in range(1, PACK)]
+        y = hidden_layer("y", stationary(w1_q, PACK), xq, steps, y_bias)
 
-        w3_rows = tile("w3_rows", [P, 2 * N], U8, "w1q0_codes")
+        w3_rows = tile("w3_rows", [P, 2 * N], U8, "w1q_codes")
         nc.sync.dma_start(w3_rows[:].bitcast(I32), w3_words[0].bitcast(I32))
         res_rows = load_rows("res_rows", res, "xq_codes")
 
-        z_first = tile("z_first", [P, PACK, S // 2], BF16, 4 * T)
-        z_later = tile("z_later", [P, PACK, S // 2], BF16, "zero_bias0")
-        shuffle(z_first[:], y, s1_t, HALVES[0])
-        for t in range(2):
-            nc.vector.tensor_copy(z_later[:, t, :], y[t][:].indirect(entries(s1_t, HALVES[1])))
-        for n, cols in enumerate(CHUNKS[1:]):
-            for t in range(2, PACK):
-                nc.vector.tensor_copy(z_later[:, t, n * PIECE : (n + 1) * PIECE], y[t][:].indirect(entries(s1_t, cols)))
-        z = [z_first[:], z_later[:, :, 0:PIECE], z_later[:, :, PIECE : 2 * PIECE]]
-        z_woven = [tile("z_woven%d" % n, [P, c.stop - c.start, PACK], BF16, ("w1_bf0", 4 * T, 4 * T + 1024)[n]) for n, c in enumerate(CHUNKS)]
-        for ts in (slice(0, 2), slice(2, 4)):
-            deal_weight(on_scalar, w2_bf[:, ts, P // 2 : P, :], w2_right[:], ts)
-        for n in range(len(CHUNKS)):
-            weave(on_scalar, z_woven[n][:], z[n])
-        w2_first, w2_rest = packed("w2q0", P), packed("w2q1", 3 * P, "zero_bias0")
+        z_planes = [tile("z_planes%d" % u, [P, PACK, S // 2], BF16, (STAGE, "y_bias")[u]) for u in range(2)]
+        shuffle(z_planes[0], y, s1_t, HALVES[0], 3)
+        shuffle(z_planes[1], y, s1_t, HALVES[1], 1)
+        nc.gpsimd.tensor_scalar(
+            w2_bf[:, :, P // 2 : P, :].rearrange("p t m j -> p m t j"),
+            w2_right[:].rearrange("p j (m t) -> p m t j", t=PACK),
+            1.0,
+            0.0,
+            MULT,
+            ADD,
+        )
+        z_woven = [
+            tile("z_woven%d" % n, [P, cols.stop - cols.start, PACK], BF16, after)
+            for n, (cols, after) in enumerate(zip(CHUNKS, ("w1_bf0", STAGE, STAGE + WOVEN)))
+        ]
+        w2_first, w2_rest = packed("w2q0", 2 * P), packed("w2q1", 2 * P)
         zq = packed("zq", S)
-        quantize(w2_first, slice(0, P), dealt(w2_bf, slice(0, 1)))
-        for n, cols in enumerate(CHUNKS):
-            quantize(zq, cols, flat(z_woven[n][:]))
-        quantize(w2_rest, slice(0, P), dealt(w2_bf, slice(1, 2)))
-        quantize(w2_rest, slice(P, 3 * P), dealt(w2_bf, slice(2, 4)))
-        h = hidden_layer("h", stationary(w2_first, w2_rest), zq, zero_bias[1][:, 0:1], 1.0)
+        weave(on_vector, z_woven[0][:], z_planes[0][:])
+        quantize(w2_first, slice(0, 2 * P), dealt(w2_bf, slice(0, 2)))
+        quantize(zq, CHUNKS[0], flat(z_woven[0][:]))
+        quantize(w2_rest, slice(0, 2 * P), dealt(w2_bf, slice(2, 4)))
+        weave(on_vector, z_woven[1][:], z_planes[1][:, :, 0:PIECE])
+        weave(on_vector, z_woven[2][:], z_planes[1][:, :, PIECE : 2 * PIECE])
+        for n in (1, 2):
+            quantize(zq, CHUNKS[n], flat(z_woven[n][:]))
+        steps = [(t, HALVES[0:1]) for t in range(PACK)] + [(0, CHUNKS[1:2]), (0, CHUNKS[2:3])]
+        steps = steps + [(t, HALVES[1:2]) for t in range(1, PACK)]
+        h = hidden_layer("h", stationary(w2_first, 2) + stationary(w2_rest, 2), zq, steps, h_bias)
 
-        w3_dealt_scales = tile("w3_dealt_scales", [P, PACK, P], U8, 4 * T + 1024)
+        w3_dealt_scales = tile("w3_dealt_scales", [P, PACK, P], U8, STAGE + WOVEN)
         nc.vector.tensor_copy(w3_dealt_scales[:], w3s[:].rearrange("p (m t) -> p t m", t=PACK))
-        w3_dealt = tile("w3_dealt", [P, PACK, P, 2], U8, 4 * T + 1536)
+        w3_dealt = tile("w3_dealt", [P, PACK, P, 2], U8, STAGE + WOVEN + N)
         nc.vector.tensor_copy(
             w3_dealt[:].rearrange("p t m b -> p (t m b)").bitcast(U16).rearrange("p (t m) -> p t m", t=PACK),
             w3_rows[:].bitcast(U16).rearrange("p (m t) -> p t m", t=PACK),
@@ -185,7 +205,7 @@ def tile_picked_shuf3_silu_po_kernel(
         pieces = [slice(c0, c0 + PIECE) for c0 in range(0, S, PIECE)]
         z2_planes = [
             tile("z2_%d" % n, [P, PACK, cols.stop - cols.start], BF16, after)
-            for n, (cols, after) in enumerate(zip(CHUNKS[:2], (None, "zero_bias1")))
+            for n, (cols, after) in enumerate(zip(CHUNKS[:2], (None, "h_bias")))
         ]
         z2_woven = [tile("z2_woven%d" % n, [P, PIECE, PACK], BF16) for n in range(len(pieces))]
         out_woven = [tile("out_woven%d" % n, [P, c.stop - c.start, PACK], BF16) for n, c in enumerate(CHUNKS)]
@@ -196,11 +216,11 @@ def tile_picked_shuf3_silu_po_kernel(
             return (slice(0, 2), slice(2, 4)) if n == len(pieces) - 1 else (slice(0, PACK),)
 
         def multiply(n):
-            z2q = packed("z2q%d" % n, PIECE)
+            z2q = packed("z2q%d" % n, PIECE, "z2q0_codes" if n == len(pieces) - 1 else None)
             quantize(z2q, slice(0, PIECE), flat(z2_woven[n][:]))
             sums[n] = []
             for planes in plane_groups(n):
-                acc = bank("out_acc%d_%d" % (n, planes.start), (n + planes.start) % PACK, [P, planes.stop - planes.start, PIECE])
+                acc = bank("out_acc%d_%d" % (n, planes.start), [P, planes.stop - planes.start, PIECE])
                 sums[n].append(acc)
                 for t in range(planes.start, planes.stop):
                     nc.tensor.matmul_mx(
@@ -225,15 +245,15 @@ def tile_picked_shuf3_silu_po_kernel(
         def store_words(cols):
             nc.sync.dma_start(out_words[:, cols], out_q[0][:, cols].bitcast(I32))
 
+        shuffle(z2_planes[0], h, s2_t, CHUNKS[0], 3)
+        shuffle(z2_planes[1], h, s2_t, CHUNKS[1], 1)
         for n in range(2):
-            shuffle(z2_planes[n][:], h, s2_t, CHUNKS[n])
-        for n in range(2):
-            weave(on_scalar, z2_woven[n][:], z2_planes[0][:, :, pieces[n]])
+            weave(on_vector, z2_woven[n][:], z2_planes[0][:, :, pieces[n]])
         multiply(0)
         multiply(1)
+        weave(on_vector, z2_woven[2][:], z2_planes[1][:])
         z2_last = tile("z2_2", [P, PACK, PIECE], BF16, "z2_0")
-        shuffle(z2_last[:], h, s2_t, CHUNKS[2])
-        weave(on_scalar, z2_woven[2][:], z2_planes[1][:])
+        shuffle(z2_last, h, s2_t, CHUNKS[2], 1)
         weave(on_scalar, z2_woven[3][:], z2_last[:])
         multiply(2)
         add_residual(0)

@@ -17,7 +17,6 @@ SILU = mybir.ActivationFunctionType.Silu
 COPY = mybir.ActivationFunctionType.Copy
 ADD = mybir.AluOpType.add
 MULT = mybir.AluOpType.mult
-ALONG_ROW = mybir.AxisListType.X
 
 P = 128
 PACK = 4
@@ -125,23 +124,30 @@ def tile_picked_shuf3_silu_po_kernel(
         def dealt(pair, ts):
             return pair[:, ts, :, :].rearrange("p t m j -> p (t m j)")
 
+        staged = tile("xs_staged", [P, 2, T // 4], I32)
+        for u in range(2):
+            rows = x_scales[0, 2 * PACK * u : 2 * PACK * (u + 1), :].rearrange("(q r) c -> r q c", q=2)
+            nc.sync.dma_start(staged[P // 2 * u : P // 2 * u + PACK, :, :], rows.bitcast(I32))
         offs_t = load_list("offs_t", offs)
         w1_rows = load_rows("w1_rows", w1, None)
-        xs = load_scales("xs", x_scales, nc.scalar)
-        s1_t = load_list("s1_t", s1)
-        s2_t = load_list("s2_t", s2)
-        zeros = tile("zeros", [P, 2, GROUP], F32, STAGE - 4 * GROUP)
-        nc.vector.memset(zeros[:], 0.0)
-        y_bias, h_bias = tile("y_bias", [P, 1], F32), tile("h_bias", [P, 1], F32)
-        nc.vector.tensor_reduce(y_bias[:], zeros[:, 0, :], ALONG_ROW, ADD)
-        nc.vector.tensor_reduce(h_bias[:], zeros[:, 1, :], ALONG_ROW, ADD)
+        xs = tile("xs", [P, T], U8)
+        nc.vector.memset(xs[:].bitcast(I32), 0)
+        for q in range(P // QUADRANT):
+            first = P // 2 * (q // 2)
+            live = xs[QUADRANT * q : QUADRANT * q + PACK, :]
+            nc.vector.tensor_copy(live.bitcast(I32), staged[first : first + PACK, q % 2, :])
         xw = tile("xw", [P, T], I32, 0)
         nc.sync.dma_start(xw[:], x_words[0].rearrange("p c r -> p (c r)").bitcast(I32))
+        w2_left = load_rows("w2_left", w2[:, 0 : H // 2], STAGE)
+        s1_t = load_list("s1_t", s1)
+        s2_t = load_list("s2_t", s2)
+        y_bias, h_bias = tile("y_bias", [P, 1], F32), tile("h_bias", [P, 1], F32)
+        nc.vector.memset(h_bias[:], 0.0)
+        nc.scalar.activation(y_bias[:], h_bias[:], SILU)
 
         w1_bf = [tile("w1_bf%d" % u, [P, 2, P, PACK], BF16) for u in range(2)]
         deal_weight(on_vector, w1_bf[0][:], w1_rows[:], slice(0, 2))
         deal_weight(on_scalar, w1_bf[1][:], w1_rows[:], slice(2, 4))
-        w2_left = load_rows("w2_left", w2[:, 0 : H // 2], STAGE)
         xq = packed("xq", S)
         nc.vector.tensor_copy(xq[1][:], xs[:].indirect(offs_t[:]))
         w1_q = packed("w1q", PACK * P)

@@ -76,6 +76,10 @@ def tile_picked_shuf3_silu_po_kernel(
         def deal_weight(copy, dealt, rows, tiles):
             copy(dealt.rearrange("p t m j -> p m j t"), rows.rearrange("p j (m t) -> p m j t", t=PACK)[:, :, :, tiles])
 
+        def deal_on_gpsimd(dealt, rows):
+            walk = rows.rearrange("p j (m t) -> p m t j", t=PACK)
+            nc.gpsimd.tensor_scalar(dealt.rearrange("p t m j -> p m t j"), walk, 1.0, 0.0, MULT, ADD)
+
         def packed(name, width, after=None):
             return tile(name + "_codes", [P, width], U32, after), tile(name + "_scales", [P, width], U8)
 
@@ -141,6 +145,8 @@ def tile_picked_shuf3_silu_po_kernel(
         w2_left = load_rows("w2_left", w2[:, 0 : H // 2], STAGE)
         s1_t = load_list("s1_t", s1)
         s2_t = load_list("s2_t", s2)
+        w2_right = load_rows("w2_right", w2[:, H // 2 : H], None)
+        w3s = load_scales("w3s", w3_scales, nc.sync)
         y_bias, h_bias = tile("y_bias", [P, 1], F32), tile("h_bias", [P, 1], F32)
         nc.vector.memset(h_bias[:], 0.0)
         nc.scalar.activation(y_bias[:], h_bias[:], SILU)
@@ -153,13 +159,11 @@ def tile_picked_shuf3_silu_po_kernel(
         w1_q = packed("w1q", PACK * P)
         for u in range(2):
             quantize(w1_q, slice(2 * u * P, 2 * (u + 1) * P), dealt(w1_bf[u], slice(0, 2)))
-        w2_right = load_rows("w2_right", w2[:, H // 2 : H], "w1_bf0")
         for cols in PICKS:
             nc.vector.tensor_copy(xq[0][:, cols], xw[:].bitcast(U32).indirect(entries(offs_t, cols)))
-        w3s = load_scales("w3s", w3_scales, nc.sync, 0)
         w2_bf = tile("w2_bf", [P, PACK, P, PACK], BF16)
-        for ts in (slice(0, 2), slice(2, 4)):
-            deal_weight(on_vector, w2_bf[:, ts, 0 : P // 2, :], w2_left[:], ts)
+        deal_on_gpsimd(w2_bf[:, :, 0 : P // 2, :], w2_left[:])
+        deal_on_gpsimd(w2_bf[:, :, P // 2 : P, :], w2_right[:])
         steps = [(t, PICKS[0:1]) for t in range(PACK)] + [(0, PICKS[1:2]), (0, PICKS[2:3])]
         steps = steps + [(t, PICKS[1:3]) for t in range(1, PACK)]
         y = hidden_layer("y", stationary(w1_q, PACK), xq, steps, y_bias)
@@ -168,20 +172,12 @@ def tile_picked_shuf3_silu_po_kernel(
         nc.sync.dma_start(w3_rows[:].bitcast(I32), w3_words[0].bitcast(I32))
         res_rows = load_rows("res_rows", res, "xq_codes")
 
-        z_planes = [tile("z_planes%d" % u, [P, PACK, S // 2], BF16, (STAGE, "y_bias")[u]) for u in range(2)]
+        z_planes = [tile("z_planes%d" % u, [P, PACK, S // 2], BF16, (STAGE + 4 * WOVEN, "y_bias")[u]) for u in range(2)]
         shuffle(z_planes[0], y, s1_t, HALVES[0], 3)
         shuffle(z_planes[1], y, s1_t, HALVES[1], 1)
-        nc.gpsimd.tensor_scalar(
-            w2_bf[:, :, P // 2 : P, :].rearrange("p t m j -> p m t j"),
-            w2_right[:].rearrange("p j (m t) -> p m t j", t=PACK),
-            1.0,
-            0.0,
-            MULT,
-            ADD,
-        )
         z_woven = [
             tile("z_woven%d" % n, [P, cols.stop - cols.start, PACK], BF16, after)
-            for n, (cols, after) in enumerate(zip(CHUNKS, ("w1_bf0", STAGE, STAGE + WOVEN)))
+            for n, (cols, after) in enumerate(zip(CHUNKS, ("w2_right", STAGE + 4 * WOVEN, STAGE + 5 * WOVEN)))
         ]
         w2_first, w2_rest = packed("w2q0", 2 * P), packed("w2q1", 2 * P)
         zq = packed("zq", S)
@@ -197,9 +193,9 @@ def tile_picked_shuf3_silu_po_kernel(
         steps = steps + [(t, HALVES[1:2]) for t in range(1, PACK)]
         h = hidden_layer("h", stationary(w2_first, 2) + stationary(w2_rest, 2), zq, steps, h_bias)
 
-        w3_dealt_scales = tile("w3_dealt_scales", [P, PACK, P], U8, STAGE + WOVEN)
+        w3_dealt_scales = tile("w3_dealt_scales", [P, PACK, P], U8, STAGE + 5 * WOVEN)
         nc.vector.tensor_copy(w3_dealt_scales[:], w3s[:].rearrange("p (m t) -> p t m", t=PACK))
-        w3_dealt = tile("w3_dealt", [P, PACK, P, 2], U8, STAGE + WOVEN + N)
+        w3_dealt = tile("w3_dealt", [P, PACK, P, 2], U8, STAGE + 5 * WOVEN + N)
         nc.vector.tensor_copy(
             w3_dealt[:].rearrange("p t m b -> p (t m b)").bitcast(U16).rearrange("p (t m) -> p t m", t=PACK),
             w3_rows[:].bitcast(U16).rearrange("p (m t) -> p t m", t=PACK),

from contextlib import ExitStack

import concourse.mybir as mybir

K, T, S, N, H = 512, 2048, 512, 512, 512
FLOPS = 2 * S * (K * H + H * H + H * N)

F32 = mybir.dt.float32
BF16 = mybir.dt.bfloat16
I32 = mybir.dt.int32
U32 = mybir.dt.uint32
U16 = mybir.dt.uint16
U8 = mybir.dt.uint8
FP8X4 = mybir.dt.float8_e4m3fn_x4
FP4X4 = mybir.dt.float4_e2m1fn_x4
SILU = mybir.ActivationFunctionType.Silu
COPY = mybir.ActivationFunctionType.Copy
ADD = mybir.AluOpType.add
MULT = mybir.AluOpType.mult

P = 128
PACK = 4
GROUP = 16
QUADRANT = 32
PIECE = 128
HALVES = (slice(0, S // 2), slice(S // 2, S))
CHUNKS = (slice(0, 256), slice(256, 384), slice(384, 512))
PICKS = (slice(0, 128), slice(128, 384), slice(384, 512))
RUN = 4
STAGE = 4 * T
WOVEN = 2 * PACK * PIECE


def tile_picked_shuf3_silu_po_kernel(
    tc, x_words, x_scales, w1, w2, res, w3_words, w3_scales, offs, s1, s2, out_0, out_1, out_2
):
    nc = tc.nc
    on_scalar, on_vector = nc.scalar.copy, nc.vector.tensor_copy
    with ExitStack() as ctx:
        keep = ctx.enter_context(tc.tile_pool(name="keep", bufs=1))
        placed = ctx.enter_context(tc.tile_pool(name="placed", bufs=1))
        psum = ctx.enter_context(tc.psum_pool(name="psum", bufs=1))

        def tile(name, shape, dtype, after=None):
            if isinstance(after, int):
                return placed.tile(shape, dtype, name=name, offset=after, align_bytes=64)
            return keep.tile(shape, dtype, name=name, tag=after or name, align_bytes=64)

        banks_taken = []

        def bank(name, shape):
            banks_taken.append(name)
            return psum.tile(shape, F32, name=name, tag="bank%d" % (len(banks_taken) % 8))

        def entries(lst, cols):
            return lst[:, cols.start // GROUP : cols.stop // GROUP]

        def load_list(name, src):
            lst = keep.tile([P, S // GROUP], U16, name=name)
            nc.sync.dma_start(lst[:], src)
            return lst

        def load_rows(name, src, after):
            rows = tile(name, [P, PACK, src.shape[1]], F32, after)
            nc.sync.dma_start(rows[:], src.rearrange("(p j) c -> p j c", j=PACK))
            return rows

        def load_scales(name, src, queue, after=None):
            planes = tile(name, [P, src.shape[2]], U8, after)
            nc.vector.memset(planes[:].bitcast(I32), 0)
            for q in range(P // QUADRANT):
                live = planes[QUADRANT * q : QUADRANT * q + PACK, :]
                queue.dma_start(live.bitcast(I32), src[0, PACK * q : PACK * q + PACK, :].bitcast(I32))
            return planes

        def deal_weight(copy, dealt, rows, tiles):
            copy(dealt.rearrange("p t m j -> p m j t"), rows.rearrange("p j (m t) -> p m j t", t=PACK)[:, :, :, tiles])

        def deal_on_gpsimd(dealt, rows):
            walk = rows.rearrange("p j (m t) -> p m t j", t=PACK)
            nc.gpsimd.tensor_scalar(dealt.rearrange("p t m j -> p m t j"), walk, 1.0, 0.0, MULT, ADD)

        def packed(name, width, after=None):
            return tile(name + "_codes", [P, width], U32, after), tile(name + "_scales", [P, width], U8)

        def quantize(operand, cols, values):
            nc.vector.quantize_mx(out=operand[0][:, cols].bitcast(FP8X4), scales=operand[1][:, cols], in_=values)

        def gather_on_vector(plane, row, lst, cols):
            nc.vector.tensor_copy(plane, row[:].indirect(entries(lst, cols)))

        def gather_on_scalar(plane, row, lst, cols):
            nc.scalar.activation(plane, row[:].indirect(entries(lst, cols)), COPY)

        def shuffle(planes, rows, lst, cols, vector_planes):
            for t in range(PACK):
                gather = gather_on_vector if t < vector_planes else gather_on_scalar
                gather(planes[:, t, :], rows[t], lst, cols)

        def weave(copy, woven, planes):
            copy(woven.rearrange("p (c i) t -> p c t i", i=RUN), planes.rearrange("p t (c i) -> p c t i", i=RUN))

        def flat(woven):
            return woven.rearrange("p c t -> p (c t)")

        def hidden_layer(name, weights, moving, steps, last_bias):
            rows = [tile("%s%d" % (name, t), [P, S], F32) for t in range(PACK)]
            for n, (t, chunks) in enumerate(steps):
                first, end = chunks[0].start, chunks[-1].stop
                acc = bank("%s_acc%d" % (name, n), [P, end - first])
                for cols in chunks:
                    nc.tensor.matmul_mx(
                        out=acc[:, cols.start - first : cols.stop - first],
                        lhsT=weights[t][0].bitcast(FP8X4),
                        lhsT_scale=weights[t][1],
                        rhs=moving[0][:, cols].bitcast(FP8X4),
                        rhs_scale=moving[1][:, cols],
                        start=True,
                        stop=True,
                    )
                bias = last_bias[:] if n == len(steps) - 1 else 0.0
                nc.scalar.activation(rows[t][:, first:end], acc[:], SILU, bias=bias)
            return rows

        def stationary(operand, count):
            return [(operand[0][:, t * P : (t + 1) * P], operand[1][:, t * P : (t + 1) * P]) for t in range(count)]

        def dealt(pair, ts):
            return pair[:, ts, :, :].rearrange("p t m j -> p (t m j)")

        staged = tile("xs_staged", [P, 2, T // 4], I32)
        for u in range(2):
            rows = x_scales[0, 2 * PACK * u : 2 * PACK * (u + 1), :].rearrange("(q r) c -> r q c", q=2)
            nc.sync.dma_start(staged[P // 2 * u : P // 2 * u + PACK, :, :], rows.bitcast(I32))
        offs_t = load_list("offs_t", offs)
        w1_rows = load_rows("w1_rows", w1, None)
        xs = tile("xs", [P, T], U8)
        nc.vector.memset(xs[:].bitcast(I32), 0)
        for q in range(P // QUADRANT):
            first = P // 2 * (q // 2)
            live = xs[QUADRANT * q : QUADRANT * q + PACK, :]
            nc.vector.tensor_copy(live.bitcast(I32), staged[first : first + PACK, q % 2, :])
        xw = tile("xw", [P, T], I32, 0)
        nc.sync.dma_start(xw[:], x_words[0].rearrange("p c r -> p (c r)").bitcast(I32))
        w2_left = load_rows("w2_left", w2[:, 0 : H // 2], STAGE)
        s1_t = load_list("s1_t", s1)
        s2_t = load_list("s2_t", s2)
        w2_right = load_rows("w2_right", w2[:, H // 2 : H], None)
        w3s = load_scales("w3s", w3_scales, nc.sync)
        y_bias, h_bias = tile("y_bias", [P, 1], F32), tile("h_bias", [P, 1], F32)
        nc.vector.memset(h_bias[:], 0.0)
        nc.scalar.activation(y_bias[:], h_bias[:], SILU)

        w1_bf = [tile("w1_bf%d" % u, [P, 2, P, PACK], BF16) for u in range(2)]
        deal_weight(on_vector, w1_bf[0][:], w1_rows[:], slice(0, 2))
        deal_weight(on_scalar, w1_bf[1][:], w1_rows[:], slice(2, 4))
        xq = packed("xq", S)
        nc.vector.tensor_copy(xq[1][:], xs[:].indirect(offs_t[:]))
        w1_q = packed("w1q", PACK * P)
        for u in range(2):
            quantize(w1_q, slice(2 * u * P, 2 * (u + 1) * P), dealt(w1_bf[u], slice(0, 2)))
        for cols in PICKS:
            nc.vector.tensor_copy(xq[0][:, cols], xw[:].bitcast(U32).indirect(entries(offs_t, cols)))
        w2_bf = tile("w2_bf", [P, PACK, P, PACK], BF16)
        deal_on_gpsimd(w2_bf[:, :, 0 : P // 2, :], w2_left[:])
        deal_on_gpsimd(w2_bf[:, :, P // 2 : P, :], w2_right[:])
        steps = [(t, PICKS[0:1]) for t in range(PACK)] + [(0, PICKS[1:2]), (0, PICKS[2:3])]
        steps = steps + [(t, PICKS[1:3]) for t in range(1, PACK)]
        y = hidden_layer("y", stationary(w1_q, PACK), xq, steps, y_bias)

        w3_rows = tile("w3_rows", [P, 2 * N], U8, "w1q_codes")
        nc.sync.dma_start(w3_rows[:].bitcast(I32), w3_words[0].bitcast(I32))
        res_rows = load_rows("res_rows", res, "xq_codes")

        z_planes = [tile("z_planes%d" % u, [P, PACK, S // 2], BF16, (STAGE + 4 * WOVEN, "y_bias")[u]) for u in range(2)]
        shuffle(z_planes[0], y, s1_t, HALVES[0], 3)
        shuffle(z_planes[1], y, s1_t, HALVES[1], 1)
        z_woven = [
            tile("z_woven%d" % n, [P, cols.stop - cols.start, PACK], BF16, after)
            for n, (cols, after) in enumerate(zip(CHUNKS, ("w2_right", STAGE + 4 * WOVEN, STAGE + 5 * WOVEN)))
        ]
        w2_first, w2_rest = packed("w2q0", 2 * P), packed("w2q1", 2 * P)
        zq = packed("zq", S)
        weave(on_vector, z_woven[0][:], z_planes[0][:])
        quantize(w2_first, slice(0, 2 * P), dealt(w2_bf, slice(0, 2)))
        quantize(zq, CHUNKS[0], flat(z_woven[0][:]))
        quantize(w2_rest, slice(0, 2 * P), dealt(w2_bf, slice(2, 4)))
        weave(on_vector, z_woven[1][:], z_planes[1][:, :, 0:PIECE])
        weave(on_vector, z_woven[2][:], z_planes[1][:, :, PIECE : 2 * PIECE])
        for n in (1, 2):
            quantize(zq, CHUNKS[n], flat(z_woven[n][:]))
        steps = [(t, HALVES[0:1]) for t in range(PACK)] + [(0, CHUNKS[1:2]), (0, CHUNKS[2:3])]
        steps = steps + [(t, HALVES[1:2]) for t in range(1, PACK)]
        h = hidden_layer("h", stationary(w2_first, 2) + stationary(w2_rest, 2), zq, steps, h_bias)

        w3_dealt_scales = tile("w3_dealt_scales", [P, PACK, P], U8, STAGE + 5 * WOVEN)
        nc.vector.tensor_copy(w3_dealt_scales[:], w3s[:].rearrange("p (m t) -> p t m", t=PACK))
        w3_dealt = tile("w3_dealt", [P, PACK, P, 2], U8, STAGE + 5 * WOVEN + N)
        nc.vector.tensor_copy(
            w3_dealt[:].rearrange("p t m b -> p (t m b)").bitcast(U16).rearrange("p (t m) -> p t m", t=PACK),
            w3_rows[:].bitcast(U16).rearrange("p (m t) -> p t m", t=PACK),
        )

        out_q = packed("out_q", S)
        out_rows = out_0.rearrange("(p t) c -> p t c", t=PACK)
        out_words = out_1[0].rearrange("p c r -> p (c r)").bitcast(I32)
        pieces = [slice(c0, c0 + PIECE) for c0 in range(0, S, PIECE)]
        z2_planes = [
            tile("z2_%d" % n, [P, PACK, cols.stop - cols.start], BF16, after)
            for n, (cols, after) in enumerate(zip(CHUNKS[:2], (None, "h_bias")))
        ]
        z2_woven = [tile("z2_woven%d" % n, [P, PIECE, PACK], BF16) for n in range(len(pieces))]
        out_woven = [tile("out_woven%d" % n, [P, c.stop - c.start, PACK], BF16) for n, c in enumerate(CHUNKS)]
        out_pieces = [out_woven[0][:, 0:PIECE, :], out_woven[0][:, PIECE : 2 * PIECE, :], out_woven[1][:], out_woven[2][:]]
        sums, results = {}, {}

        def plane_groups(n):
            return (slice(0, 2), slice(2, 4)) if n == len(pieces) - 1 else (slice(0, PACK),)

        def multiply(n):
            z2q = packed("z2q%d" % n, PIECE, "z2q0_codes" if n == len(pieces) - 1 else None)
            quantize(z2q, slice(0, PIECE), flat(z2_woven[n][:]))
            sums[n] = []
            for planes in plane_groups(n):
                acc = bank("out_acc%d_%d" % (n, planes.start), [P, planes.stop - planes.start, PIECE])
                sums[n].append(acc)
                for t in range(planes.start, planes.stop):
                    nc.tensor.matmul_mx(
                        out=acc[:, t - planes.start, :],
                        lhsT=w3_dealt[:, t, :, :].rearrange("p m b -> p (m b)").bitcast(FP4X4),
                        lhsT_scale=w3_dealt_scales[:, t, :],
                        rhs=z2q[0][:].bitcast(FP8X4),
                        rhs_scale=z2q[1][:],
                        start=True,
                        stop=True,
                    )

        def add_residual(n):
            results[n] = tile("result%d" % n, [P, PACK, PIECE], F32)
            for planes, acc in zip(plane_groups(n), sums[n]):
                nc.vector.tensor_tensor(results[n][:, planes, :], acc[:], res_rows[:, planes, pieces[n]], ADD)
            nc.sync.dma_start(out_rows[:, :, pieces[n]], results[n][:])

        def hand_on(n):
            quantize(out_q, CHUNKS[n], flat(out_woven[n][:]))

        def store_words(cols):
            nc.sync.dma_start(out_words[:, cols], out_q[0][:, cols].bitcast(I32))

        shuffle(z2_planes[0], h, s2_t, CHUNKS[0], 3)
        shuffle(z2_planes[1], h, s2_t, CHUNKS[1], 1)
        for n in range(2):
            weave(on_vector, z2_woven[n][:], z2_planes[0][:, :, pieces[n]])
        multiply(0)
        multiply(1)
        weave(on_vector, z2_woven[2][:], z2_planes[1][:])
        z2_last = tile("z2_2", [P, PACK, PIECE], BF16, "z2_0")
        shuffle(z2_last, h, s2_t, CHUNKS[2], 1)
        weave(on_scalar, z2_woven[3][:], z2_last[:])
        multiply(2)
        add_residual(0)
        multiply(3)
        for n in range(1, len(pieces)):
            add_residual(n)
        for n in range(len(pieces) - 1):
            weave(on_scalar, out_pieces[n], results[n][:])
        hand_on(0)
        store_words(HALVES[0])
        weave(on_vector, out_pieces[3][:, 0 : PIECE // 2, :], results[3][:, :, 0 : PIECE // 2])
        weave(on_scalar, out_pieces[3][:, PIECE // 2 : PIECE, :], results[3][:, :, PIECE // 2 : PIECE])
        hand_on(1)
        hand_on(2)
        store_words(HALVES[1])
        for q in range(P // QUADRANT):
            queue = nc.sync if q % 2 == 0 else nc.scalar
            live = out_q[1][QUADRANT * q : QUADRANT * q + PACK, :]
            queue.dma_start(out_2[0, PACK * q : PACK * q + PACK, :].bitcast(I32), live.bitcast(I32))
